import numpy as np
import ml_dtypes


def mxq(x, axis, fmt="e4m3"):
    dtype, down = {"e4m3": (ml_dtypes.float8_e4m3fn, 7), "e5m2": (ml_dtypes.float8_e5m2, 14)}[fmt]
    v = np.moveaxis(np.asarray(x, np.float32).astype(ml_dtypes.bfloat16).astype(np.float64), axis, -1)
    blocks = v.reshape(v.shape[:-1] + (-1, 32))
    amax = np.abs(blocks).max(-1, keepdims=True)
    byte = np.maximum(np.where(amax > 0, np.frexp(amax)[1] - 1 + 127, 0) - down, 1)
    scale = np.exp2(byte - 127.0)
    codes = (blocks / scale).astype(np.float32).astype(dtype).astype(np.float64)
    return np.moveaxis((codes * scale).reshape(v.shape), -1, axis)


WIDE = False


def mx_kscale(k):
    if not WIDE:
        return np.ones(k)
    levels = np.array([10, -10, 5, -5, 0])
    if k % 512:
        return np.exp2(np.random.permutation(np.resize(levels, k // 32))).repeat(32)
    a = np.empty((k // 512, 16))
    for p in range(k // 512):
        a[p, :8] = np.random.permutation(np.resize(levels, 8))
        for g in range(8):
            far = levels[np.abs(levels - a[p, g]) >= 10]
            a[p, g + 8] = far[np.random.randint(len(far))]
    return np.exp2(a.ravel()).repeat(32)


def f64(x):
    return np.asarray(x).astype(np.float64)


def striped(idx):
    return np.tile(idx.reshape(-1, 16).T, (8, 1)).astype(np.uint16)


def unstriped(offs):
    return offs[:16].T.reshape(-1).astype(np.int64)


E2M1 = np.array([0.0, 0.5, 1.0, 1.5, 2.0, 3.0, 4.0, 6.0, -0.0, -0.5, -1.0, -1.5, -2.0, -3.0, -4.0, -6.0])


def pack_fp4(w):
    k, n = w.shape
    w = f64(np.asarray(w, np.float32).astype(ml_dtypes.bfloat16)).reshape(k // 32, 32, n)
    amax = np.abs(w).max(1)
    mant, ex = np.frexp(amax / 6.0)
    byte = np.clip(np.where(amax > 0, np.where(mant > 0.5, ex, ex - 1) + 127, 1), 1, 254)
    scaled = (w * np.exp2(127.0 - byte)[:, None, :]).reshape(k, n).astype(np.float32)
    c = np.ascontiguousarray(scaled.reshape(k // 512, 128, 4, n).transpose(0, 1, 3, 2)).astype(ml_dtypes.float4_e2m1fn).view(np.uint8) & 0xF
    words = (c[..., 0::2] | (c[..., 1::2] << 4)).reshape(k // 512, 128, 2 * n)
    return np.ascontiguousarray(words), np.ascontiguousarray(byte.astype(np.uint8).reshape(k // 512, 16, n))


def unpack_fp4(words, scales):
    g, _, n = scales.shape
    words = np.ascontiguousarray(words).reshape(g, 128, n, 2)
    nib = np.empty((g, 128, n, 4), np.uint8)
    nib[..., 0::2] = words & 0xF
    nib[..., 1::2] = words >> 4
    vals = E2M1[nib] * np.repeat(np.exp2(scales.astype(np.float64) - 127.0), 8, axis=1)[..., None]
    return vals.transpose(0, 1, 3, 2).reshape(g * 512, n)


def relu(v):
    return np.maximum(v, 0.0)


def sigmoid(v):
    return 1.0 / (1.0 + np.exp(-np.maximum(v, -700.0)))


K, T, S, V, N = 1024, 1024, 512, 256, 128


def setup_inputs():
    n = np.random.standard_normal
    s = mx_kscale(K)[:, None]
    packed_w1 = pack_fp4(n((K, N)) / np.sqrt(K) / s)
    packed_w2 = pack_fp4(n((K, N)) / np.sqrt(K) / s)
    packed_w3 = pack_fp4(n((K, N)) / np.sqrt(K) / s)
    return {
        "xT": (n((K, T)) * s).astype(np.float32),
        "w1_words": packed_w1[0],
        "w1_scales": packed_w1[1],
        "w2_words": packed_w2[0],
        "w2_scales": packed_w2[1],
        "w3_words": packed_w3[0],
        "w3_scales": packed_w3[1],
        "offs": striped(np.random.permutation(T)[:S]),
        "cen": striped(np.random.permutation(S)[:V]),
        "pos1": striped(np.random.permutation(S)[:V]),
        "pos2": striped(np.random.permutation(S)[:V]),
    }


def reference(xT, w1_words, w1_scales, w2_words, w2_scales, w3_words, w3_scales, offs, cen, pos1, pos2):
    xq = mxq(f64(xT)[:, unstriped(offs)], 0, "e4m3")
    y = unpack_fp4(w1_words, w1_scales).T @ xq
    yc = y[:, unstriped(cen)]
    e = unpack_fp4(w2_words, w2_scales).T @ xq
    h = unpack_fp4(w3_words, w3_scales).T @ xq
    z = (sigmoid(yc + e[:, unstriped(pos1)])) * h[:, unstriped(pos1)] + (sigmoid(yc + e[:, unstriped(pos2)])) * h[:, unstriped(pos2)]
    return relu(z)

@@ -1,0 +1,169 @@
+from contextlib import ExitStack
+
+import concourse.mybir as mybir
+
+K, T, S, V, N = 1024, 1024, 512, 256, 128
+FLOPS = 3 * 2 * K * S * N
+
+F32 = mybir.dt.float32
+BF16 = mybir.dt.bfloat16
+I32 = mybir.dt.int32
+U32 = mybir.dt.uint32
+U16 = mybir.dt.uint16
+U8 = mybir.dt.uint8
+FP8X4 = mybir.dt.float8_e4m3fn_x4
+FP4X4 = mybir.dt.float4_e2m1fn_x4
+ALU = mybir.AluOpType
+ACT = mybir.ActivationFunctionType
+
+P = 128
+PACK = 4
+K_PASS = P * PACK
+PASSES = K // K_PASS
+SLICE = 128
+SLICES = S // SLICE
+PER_COL = 16
+HALF = V // 2
+
+
+def tile_picked_gatedg_relu_e_kernel(
+    tc, xT, w1_words, w1_scales, w2_words, w2_scales, w3_words, w3_scales, offs, cen, pos1, pos2, out
+):
+    nc = tc.nc
+    with ExitStack() as ctx:
+        keep = ctx.enter_context(tc.tile_pool(name="keep", bufs=1))
+        psum = ctx.enter_context(tc.psum_pool(name="psum", bufs=1))
+
+        offs_sb = keep.tile([P, S // PER_COL], U16, name="offs_sb")
+        cen_sb = keep.tile([P, V // PER_COL], U16, name="cen_sb")
+        pos1_sb = keep.tile([P, V // PER_COL], U16, name="pos1_sb")
+        pos2_sb = keep.tile([P, V // PER_COL], U16, name="pos2_sb")
+        nc.sync.dma_start(offs_sb[:], offs)
+
+        planes = []
+        for g in range(PASSES):
+            rows = xT[g * K_PASS : (g + 1) * K_PASS, :].rearrange("(p j) t -> p j t", j=PACK)
+            for j in range(PACK):
+                plane = keep.tile([P, T], F32, name="plane%d" % (g * PACK + j))
+                nc.sync.dma_start(plane[:], rows[:, j, :])
+                planes.append(plane)
+
+        warm_in = keep.tile([P, 8], F32, name="warm_in")
+        warm_out = keep.tile([P, 8], F32, name="warm_out")
+        nc.vector.memset(warm_in[:], 0.0)
+        nc.scalar.activation(warm_out[:], warm_in[:], ACT.Sigmoid)
+
+        w_codes, w_scales = [], []
+        for i, words in enumerate((w1_words, w2_words, w3_words)):
+            codes = keep.tile([P, PASSES, 2 * N], U8, name="w_codes%d" % i, align_bytes=64)
+            nc.sync.dma_start(codes[:].bitcast(I32), words.rearrange("g p b -> p g b").bitcast(I32))
+            w_codes.append(codes)
+        for i, scales in enumerate((w1_scales, w2_scales, w3_scales)):
+            plane = keep.tile([P, PASSES, N], U8, name="w_scales%d" % i, align_bytes=64)
+            nc.vector.memset(plane[:].bitcast(I32), 0)
+            queue = nc.sync if i == 2 else nc.gpsimd
+            for q in range(4):
+                queue.dma_start(
+                    plane[32 * q : 32 * q + 4, :, :].bitcast(I32),
+                    scales[:, 4 * q : 4 * q + 4, :].rearrange("g r n -> r g n").bitcast(I32),
+                )
+            w_scales.append(plane)
+        nc.sync.dma_start(cen_sb[:], cen)
+        nc.sync.dma_start(pos1_sb[:], pos1)
+        nc.sync.dma_start(pos2_sb[:], pos2)
+
+        x_codes = [keep.tile([P, S], U32, name="x_codes%d" % g, align_bytes=64) for g in range(PASSES)]
+        x_scales = [keep.tile([P, S], U8, name="x_scales%d" % g, align_bytes=64) for g in range(PASSES)]
+        pairs = [keep.tile([P, 2, S], F32, name="pair%d" % u) for u in range(2 * PASSES)]
+        y_banks = [psum.tile([P, SLICE], F32, name="y_bank%d" % s) for s in range(SLICES)]
+        e_bank = psum.tile([P, S], F32, name="e_bank")
+        h_bank = psum.tile([P, S], F32, name="h_bank")
+
+        def gather(j, a, b):
+            nc.vector.tensor_copy(
+                pairs[j // 2][:, j % 2, a:b], planes[j][:].indirect(offs_sb[:, a // PER_COL : b // PER_COL])
+            )
+
+        def weave(dst, u, a, b):
+            nc.scalar.copy(dst[:, :, 2 * (u % 2) : 2 * (u % 2) + 2], pairs[u][:, :, a:b].rearrange("p e n -> p n e"))
+
+        def quantize(src, g, a, b):
+            nc.vector.quantize_mx(
+                out=x_codes[g][:, a:b].bitcast(FP8X4),
+                scales=x_scales[g][:, a:b],
+                in_=src[:].rearrange("p n t -> p (n t)"),
+            )
+
+        def product(bank, i, g, a, b):
+            nc.tensor.matmul_mx(
+                out=bank[:],
+                lhsT=w_codes[i][:, g, :].bitcast(FP4X4),
+                lhsT_scale=w_scales[i][:, g, :],
+                rhs=x_codes[g][:, a:b].bitcast(FP8X4),
+                rhs_scale=x_scales[g][:, a:b],
+                start=(g == 0),
+                stop=(g == PASSES - 1),
+            )
+
+        first = keep.tile([P, S, PACK], BF16, name="first", align_bytes=64)
+        for u in range(2):
+            gather(2 * u, 0, S)
+            gather(2 * u + 1, 0, S)
+            weave(first, u, 0, S)
+        quantize(first, 0, 0, S)
+        for s in range(SLICES):
+            product(y_banks[s], 0, 0, s * SLICE, (s + 1) * SLICE)
+        product(e_bank, 1, 0, 0, S)
+        product(h_bank, 2, 0, 0, S)
+
+        second = [keep.tile([P, SLICE, PACK], BF16, name="second%d" % s, align_bytes=64) for s in range(SLICES)]
+        gather(4, 0, S)
+        gather(5, 0, S)
+        for s in range(SLICES):
+            weave(second[s], 2, s * SLICE, (s + 1) * SLICE)
+        gather(6, 0, S)
+        for s in range(SLICES):
+            gather(7, s * SLICE, (s + 1) * SLICE)
+        for s in range(SLICES):
+            weave(second[s], 3, s * SLICE, (s + 1) * SLICE)
+        for s in range(SLICES):
+            quantize(second[s], 1, s * SLICE, (s + 1) * SLICE)
+            product(y_banks[s], 0, 1, s * SLICE, (s + 1) * SLICE)
+        product(e_bank, 1, 1, 0, S)
+        product(h_bank, 2, 1, 0, S)
+
+        y_sb = keep.tile([P, S], F32, name="y_sb")
+        e_sb = keep.tile([P, S], F32, name="e_sb")
+        h_sb = keep.tile([P, S], F32, name="h_sb")
+        for s in range(SLICES):
+            nc.scalar.copy(y_sb[:, s * SLICE : (s + 1) * SLICE], y_banks[s][:])
+        nc.scalar.copy(e_sb[:], e_bank[:])
+        nc.scalar.copy(h_sb[:], h_bank[:])
+
+        yc = keep.tile([P, V], F32, name="yc")
+        nc.vector.tensor_copy(yc[:], y_sb[:].indirect(cen_sb[:]))
+        gates = []
+        for d, pos in enumerate((pos1_sb, pos2_sb)):
+            both = keep.tile([P, V], F32, name="both%d" % d)
+            gate = keep.tile([P, V], F32, name="gate%d" % d)
+            nc.vector.tensor_tensor(both[:], e_sb[:].indirect(pos[:]), yc[:], ALU.add)
+            nc.scalar.activation(gate[:], both[:], ACT.Sigmoid)
+            gates.append(gate)
+        passed1 = keep.tile([P, V], F32, name="passed1")
+        nc.vector.tensor_tensor(passed1[:], h_sb[:].indirect(pos1_sb[:]), gates[0][:], ALU.mult)
+        passed2 = [keep.tile([P, HALF], F32, name="passed2_%d" % c) for c in range(2)]
+        total = [keep.tile([P, HALF], F32, name="total%d" % c) for c in range(2)]
+        result = [keep.tile([P, HALF], F32, name="result%d" % c) for c in range(2)]
+        for c in range(2):
+            cols = slice(c * HALF, (c + 1) * HALF)
+            nc.vector.tensor_tensor(
+                passed2[c][:],
+                h_sb[:].indirect(pos2_sb[:, c * HALF // PER_COL : (c + 1) * HALF // PER_COL]),
+                gates[1][:, cols],
+                ALU.mult,
+            )
+        for c in range(2):
+            nc.vector.tensor_tensor(total[c][:], passed1[:, c * HALF : (c + 1) * HALF], passed2[c][:], ALU.add)
+        for c in range(2):
+            nc.vector.tensor_scalar_max(result[c][:], total[c][:], 0.0)
+            nc.sync.dma_start(out[:, c * HALF : (c + 1) * HALF], result[c][:])

@@ -40,40 +40,48 @@ def tile_picked_gatedg_relu_e_kernel(
         pos2_sb = keep.tile([P, V // PER_COL], U16, name="pos2_sb")
         nc.sync.dma_start(offs_sb[:], offs)
 
-        planes = []
-        for g in range(PASSES):
+        planes = [
+            keep.tile([P, T], F32, name="plane%d" % j, tag="plane%d" % j, align_bytes=64) for j in range(PASSES * PACK)
+        ]
+
+        def load_plane(j):
+            g = j // PACK
             rows = xT[g * K_PASS : (g + 1) * K_PASS, :].rearrange("(p j) t -> p j t", j=PACK)
-            for j in range(PACK):
-                plane = keep.tile([P, T], F32, name="plane%d" % (g * PACK + j))
-                nc.sync.dma_start(plane[:], rows[:, j, :])
-                planes.append(plane)
+            nc.sync.dma_start(planes[j][:], rows[:, j % PACK, :])
+
+        staged = keep.tile([16, 3, PASSES, N], U8, name="staged")
+        w_scales = keep.tile([P, 3, PASSES, N], U8, name="w_scales", align_bytes=64)
+        shared = keep.tile([P, S + 2 * N], U8, name="shared", align_bytes=64)
+        w_codes = [shared[:, S - 2 * N :].rearrange("p (g b) -> p g b", g=PASSES)]
+        w_codes += [keep.tile([P, PASSES, 2 * N], U8, name="w_codes%d" % i, align_bytes=64)[:] for i in (1, 2)]
+        nc.vector.memset(w_scales[:].bitcast(I32), 0)
+
+        load_plane(0)
+        for i, scales in enumerate((w1_scales, w2_scales, w3_scales)):
+            nc.sync.dma_start(staged[:, i, :, :].bitcast(I32), scales.rearrange("g r n -> r g n").bitcast(I32))
+        for j in range(1, 6):
+            load_plane(j)
+        for q in range(4):
+            nc.sync.dma_start(
+                w_scales[32 * q : 32 * q + 4].rearrange("r i g n -> r (i g n)").bitcast(I32),
+                staged[4 * q : 4 * q + 4].rearrange("r i g n -> r (i g n)").bitcast(I32),
+            )
+        for j in range(6, 8):
+            load_plane(j)
+        for i in (1, 2, 0):
+            words = (w1_words, w2_words, w3_words)[i]
+            nc.sync.dma_start(w_codes[i].bitcast(I32), words.rearrange("g p b -> p g b").bitcast(I32))
+        nc.sync.dma_start(cen_sb[:], cen)
+        nc.sync.dma_start(pos1_sb[:], pos1)
+        nc.sync.dma_start(pos2_sb[:], pos2)
 
         warm_in = keep.tile([P, 8], F32, name="warm_in")
         warm_out = keep.tile([P, 8], F32, name="warm_out")
         nc.vector.memset(warm_in[:], 0.0)
         nc.scalar.activation(warm_out[:], warm_in[:], ACT.Sigmoid)
 
-        w_codes, w_scales = [], []
-        for i, words in enumerate((w1_words, w2_words, w3_words)):
-            codes = keep.tile([P, PASSES, 2 * N], U8, name="w_codes%d" % i, align_bytes=64)
-            nc.sync.dma_start(codes[:].bitcast(I32), words.rearrange("g p b -> p g b").bitcast(I32))
-            w_codes.append(codes)
-        for i, scales in enumerate((w1_scales, w2_scales, w3_scales)):
-            plane = keep.tile([P, PASSES, N], U8, name="w_scales%d" % i, align_bytes=64)
-            nc.vector.memset(plane[:].bitcast(I32), 0)
-            queue = nc.sync if i == 2 else nc.gpsimd
-            for q in range(4):
-                queue.dma_start(
-                    plane[32 * q : 32 * q + 4, :, :].bitcast(I32),
-                    scales[:, 4 * q : 4 * q + 4, :].rearrange("g r n -> r g n").bitcast(I32),
-                )
-            w_scales.append(plane)
-        nc.sync.dma_start(cen_sb[:], cen)
-        nc.sync.dma_start(pos1_sb[:], pos1)
-        nc.sync.dma_start(pos2_sb[:], pos2)
-
-        x_codes = [keep.tile([P, S], U32, name="x_codes%d" % g, align_bytes=64) for g in range(PASSES)]
-        x_scales = [keep.tile([P, S], U8, name="x_scales%d" % g, align_bytes=64) for g in range(PASSES)]
+        x_codes = [None, keep.tile([P, S], U32, name="x_codes1", align_bytes=64)]
+        x_scales = [keep.tile([P, S], U8, name="x_scales0", align_bytes=64)[:], shared[:, :S]]
         pairs = [keep.tile([P, 2, S], F32, name="pair%d" % u) for u in range(2 * PASSES)]
         y_banks = [psum.tile([P, SLICE], F32, name="y_bank%d" % s) for s in range(SLICES)]
         e_bank = psum.tile([P, S], F32, name="e_bank")
@@ -84,6 +92,11 @@ def tile_picked_gatedg_relu_e_kernel(
                 pairs[j // 2][:, j % 2, a:b], planes[j][:].indirect(offs_sb[:, a // PER_COL : b // PER_COL])
             )
 
+        def gather_in_place(dst, j, a, b):
+            nc.vector.tensor_copy(
+                dst[:, a:b, j % PACK], planes[j][:].indirect(offs_sb[:, a // PER_COL : b // PER_COL])
+            )
+
         def weave(dst, u, a, b):
             nc.scalar.copy(dst[:, :, 2 * (u % 2) : 2 * (u % 2) + 2], pairs[u][:, :, a:b].rearrange("p e n -> p n e"))
 
@@ -91,14 +104,14 @@ def tile_picked_gatedg_relu_e_kernel(
             nc.vector.quantize_mx(
                 out=x_codes[g][:, a:b].bitcast(FP8X4),
                 scales=x_scales[g][:, a:b],
-                in_=src[:].rearrange("p n t -> p (n t)"),
+                in_=src.rearrange("p n t -> p (n t)"),
             )
 
         def product(bank, i, g, a, b):
             nc.tensor.matmul_mx(
                 out=bank[:],
                 lhsT=w_codes[i][:, g, :].bitcast(FP4X4),
-                lhsT_scale=w_scales[i][:, g, :],
+                lhsT_scale=w_scales[:, i, g, :],
                 rhs=x_codes[g][:, a:b].bitcast(FP8X4),
                 rhs_scale=x_scales[g][:, a:b],
                 start=(g == 0),
@@ -110,24 +123,29 @@ def tile_picked_gatedg_relu_e_kernel(
             gather(2 * u, 0, S)
             gather(2 * u + 1, 0, S)
             weave(first, u, 0, S)
-        quantize(first, 0, 0, S)
-        for s in range(SLICES):
-            product(y_banks[s], 0, 0, s * SLICE, (s + 1) * SLICE)
-        product(e_bank, 1, 0, 0, S)
-        product(h_bank, 2, 0, 0, S)
 
-        second = [keep.tile([P, SLICE, PACK], BF16, name="second%d" % s, align_bytes=64) for s in range(SLICES)]
+        spans = [(0, 2 * SLICE), (2 * SLICE, 3 * SLICE), (3 * SLICE, S)]
+        second = [keep.tile([P, b - a, PACK], BF16, name="second%d" % a, align_bytes=64) for a, b in spans]
         gather(4, 0, S)
         gather(5, 0, S)
+        x_codes[0] = keep.tile([P, S], U32, name="x_codes0", tag="plane5", align_bytes=64)
+        quantize(first[:], 0, 0, S)
+        product(e_bank, 1, 0, 0, S)
+        product(h_bank, 2, 0, 0, S)
         for s in range(SLICES):
-            weave(second[s], 2, s * SLICE, (s + 1) * SLICE)
-        gather(6, 0, S)
+            product(y_banks[s], 0, 0, s * SLICE, (s + 1) * SLICE)
+        for dst, (a, b) in reversed(list(zip(second, spans))):
+            weave(dst, 2, a, b)
+        gather(6, 2 * SLICE, S)
+        gather_in_place(second[0], 6, *spans[0])
+        for dst, (a, b) in zip(second[1:], spans[1:]):
+            gather(7, a, b)
+            weave(dst, 3, a, b)
+        for s in range(2):
+            gather_in_place(second[0], 7, s * SLICE, (s + 1) * SLICE)
+        sources = [second[0][:, :SLICE, :], second[0][:, SLICE:, :], second[1][:], second[2][:]]
         for s in range(SLICES):
-            gather(7, s * SLICE, (s + 1) * SLICE)
-        for s in range(SLICES):
-            weave(second[s], 3, s * SLICE, (s + 1) * SLICE)
-        for s in range(SLICES):
-            quantize(second[s], 1, s * SLICE, (s + 1) * SLICE)
+            quantize(sources[s], 1, s * SLICE, (s + 1) * SLICE)
             product(y_banks[s], 0, 1, s * SLICE, (s + 1) * SLICE)
         product(e_bank, 1, 1, 0, S)
         product(h_bank, 2, 1, 0, S)
@@ -135,18 +153,24 @@ def tile_picked_gatedg_relu_e_kernel(
         y_sb = keep.tile([P, S], F32, name="y_sb")
         e_sb = keep.tile([P, S], F32, name="e_sb")
         h_sb = keep.tile([P, S], F32, name="h_sb")
-        for s in range(SLICES):
+        for s in range(SLICES - 1):
             nc.scalar.copy(y_sb[:, s * SLICE : (s + 1) * SLICE], y_banks[s][:])
+        nc.vector.tensor_copy(y_sb[:, S - SLICE :], y_banks[SLICES - 1][:])
         nc.scalar.copy(e_sb[:], e_bank[:])
         nc.scalar.copy(h_sb[:], h_bank[:])
 
         yc = keep.tile([P, V], F32, name="yc")
-        nc.vector.tensor_copy(yc[:], y_sb[:].indirect(cen_sb[:]))
+        halves = [(0, HALF), (HALF, V)]
+        for a, b in halves:
+            nc.vector.tensor_copy(yc[:, a:b], y_sb[:].indirect(cen_sb[:, a // PER_COL : b // PER_COL]))
         gates = []
         for d, pos in enumerate((pos1_sb, pos2_sb)):
             both = keep.tile([P, V], F32, name="both%d" % d)
             gate = keep.tile([P, V], F32, name="gate%d" % d)
-            nc.vector.tensor_tensor(both[:], e_sb[:].indirect(pos[:]), yc[:], ALU.add)
+            for a, b in halves if d == 0 else [(0, V)]:
+                nc.vector.tensor_tensor(
+                    both[:, a:b], e_sb[:].indirect(pos[:, a // PER_COL : b // PER_COL]), yc[:, a:b], ALU.add
+                )
             nc.scalar.activation(gate[:], both[:], ACT.Sigmoid)
             gates.append(gate)
         passed1 = keep.tile([P, V], F32, name="passed1")

@@ -51,8 +51,8 @@ def tile_picked_gatedg_relu_e_kernel(
 
         staged = keep.tile([16, 3, PASSES, N], U8, name="staged")
         w_scales = keep.tile([P, 3, PASSES, N], U8, name="w_scales", align_bytes=64)
-        shared = keep.tile([P, S + 2 * N], U8, name="shared", align_bytes=64)
-        w_codes = [shared[:, S - 2 * N :].rearrange("p (g b) -> p g b", g=PASSES)]
+        shared = keep.tile([P, 192 + 2 * 320], U8, name="shared", align_bytes=64)
+        w_codes = [shared[:, 192:].rearrange("p (g b) -> p g b", g=PASSES)[:, :, : 2 * N]]
         w_codes += [keep.tile([P, PASSES, 2 * N], U8, name="w_codes%d" % i, align_bytes=64)[:] for i in (1, 2)]
         nc.vector.memset(w_scales[:].bitcast(I32), 0)
 
@@ -82,7 +82,7 @@ def tile_picked_gatedg_relu_e_kernel(
 
         x_codes = [None, keep.tile([P, S], U32, name="x_codes1", align_bytes=64)]
         x_scales = [keep.tile([P, S], U8, name="x_scales0", align_bytes=64)[:], shared[:, :S]]
-        pairs = [keep.tile([P, 2, S], F32, name="pair%d" % u) for u in range(2 * PASSES)]
+        pairs = {u: keep.tile([P, 2, S], F32, name="pair%d" % u) for u in (0, 1, 3)}
         y_banks = [psum.tile([P, SLICE], F32, name="y_bank%d" % s) for s in range(SLICES)]
         e_bank = psum.tile([P, S], F32, name="e_bank")
         h_bank = psum.tile([P, S], F32, name="h_bank")
@@ -90,11 +90,6 @@ def tile_picked_gatedg_relu_e_kernel(
         def gather(j, a, b):
             nc.vector.tensor_copy(
                 pairs[j // 2][:, j % 2, a:b], planes[j][:].indirect(offs_sb[:, a // PER_COL : b // PER_COL])
-            )
-
-        def gather_in_place(dst, j, a, b):
-            nc.vector.tensor_copy(
-                dst[:, a:b, j % PACK], planes[j][:].indirect(offs_sb[:, a // PER_COL : b // PER_COL])
             )
 
         def weave(dst, u, a, b):
@@ -124,38 +119,40 @@ def tile_picked_gatedg_relu_e_kernel(
             gather(2 * u + 1, 0, S)
             weave(first, u, 0, S)
 
-        spans = [(0, 2 * SLICE), (2 * SLICE, 3 * SLICE), (3 * SLICE, S)]
+        spans = [(s * SLICE, (s + 1) * SLICE) for s in range(SLICES)]
         second = [keep.tile([P, b - a, PACK], BF16, name="second%d" % a, align_bytes=64) for a, b in spans]
+        rounded = keep.tile([P, T], BF16, name="rounded", align_bytes=64)
+        pairs[2] = keep.tile([P, 2, S], BF16, name="pair2_rounded")
         gather(4, 0, S)
-        gather(5, 0, S)
+        nc.vector.tensor_copy(rounded[:], planes[5][:])
+        nc.scalar.activation(pairs[2][:, 1, :], rounded[:].indirect(offs_sb[:]), ACT.Copy)
         x_codes[0] = keep.tile([P, S], U32, name="x_codes0", tag="plane5", align_bytes=64)
         quantize(first[:], 0, 0, S)
         product(e_bank, 1, 0, 0, S)
         product(h_bank, 2, 0, 0, S)
         for s in range(SLICES):
             product(y_banks[s], 0, 0, s * SLICE, (s + 1) * SLICE)
-        for dst, (a, b) in reversed(list(zip(second, spans))):
+        for dst, (a, b) in zip(second, spans):
             weave(dst, 2, a, b)
-        gather(6, 2 * SLICE, S)
-        gather_in_place(second[0], 6, *spans[0])
-        for dst, (a, b) in zip(second[1:], spans[1:]):
+        gather(6, 0, S - SLICE)
+        whole = second[SLICES - 1]
+        last = offs_sb[:, (S - SLICE) // PER_COL :]
+        nc.vector.tensor_copy(whole[:, :, 2], planes[6][:].indirect(last))
+        for dst, (a, b) in zip(second[:-1], spans[:-1]):
             gather(7, a, b)
             weave(dst, 3, a, b)
-        for s in range(2):
-            gather_in_place(second[0], 7, s * SLICE, (s + 1) * SLICE)
-        sources = [second[0][:, :SLICE, :], second[0][:, SLICE:, :], second[1][:], second[2][:]]
-        for s in range(SLICES):
-            quantize(sources[s], 1, s * SLICE, (s + 1) * SLICE)
-            product(y_banks[s], 0, 1, s * SLICE, (s + 1) * SLICE)
+        nc.vector.tensor_copy(whole[:, :, 3], planes[7][:].indirect(last))
+        for s in (0, 3, 1, 2):
+            quantize(second[s][:], 1, *spans[s])
+            product(y_banks[s], 0, 1, *spans[s])
         product(e_bank, 1, 1, 0, S)
         product(h_bank, 2, 1, 0, S)
 
         y_sb = keep.tile([P, S], F32, name="y_sb")
         e_sb = keep.tile([P, S], F32, name="e_sb")
         h_sb = keep.tile([P, S], F32, name="h_sb")
-        for s in range(SLICES - 1):
+        for s in (0, 3, 1, 2):
             nc.scalar.copy(y_sb[:, s * SLICE : (s + 1) * SLICE], y_banks[s][:])
-        nc.vector.tensor_copy(y_sb[:, S - SLICE :], y_banks[SLICES - 1][:])
         nc.scalar.copy(e_sb[:], e_bank[:])
         nc.scalar.copy(h_sb[:], h_bank[:])
 

@@ -66,11 +66,12 @@ def tile_picked_gatedg_relu_e_kernel(
                 w_scales[32 * q : 32 * q + 4].rearrange("r i g n -> r (i g n)").bitcast(I32),
                 staged[4 * q : 4 * q + 4].rearrange("r i g n -> r (i g n)").bitcast(I32),
             )
-        for j in range(6, 8):
-            load_plane(j)
+        load_plane(6)
         for i in (1, 2, 0):
             words = (w1_words, w2_words, w3_words)[i]
             nc.sync.dma_start(w_codes[i].bitcast(I32), words.rearrange("g p b -> p g b").bitcast(I32))
+            if i == 1:
+                load_plane(7)
         nc.sync.dma_start(cen_sb[:], cen)
         nc.sync.dma_start(pos1_sb[:], pos1)
         nc.sync.dma_start(pos2_sb[:], pos2)
@@ -114,26 +115,34 @@ def tile_picked_gatedg_relu_e_kernel(
             )
 
         first = keep.tile([P, S, PACK], BF16, name="first", align_bytes=64)
-        for u in range(2):
-            gather(2 * u, 0, S)
-            gather(2 * u + 1, 0, S)
-            weave(first, u, 0, S)
+        gather(0, 0, S)
+        gather(1, 0, S)
+        weave(first, 0, 0, S)
+        gather(2, 0, S)
+        gather(3, 0, S)
+        weave(first[:, :320, :], 1, 0, 320)
+        nc.gpsimd.tensor_copy(first[:, 320:, 2:4], pairs[1][:, :, 320:].rearrange("p e n -> p n e"))
 
         spans = [(s * SLICE, (s + 1) * SLICE) for s in range(SLICES)]
         second = [keep.tile([P, b - a, PACK], BF16, name="second%d" % a, align_bytes=64) for a, b in spans]
         rounded = keep.tile([P, T], BF16, name="rounded", align_bytes=64)
         pairs[2] = keep.tile([P, 2, S], BF16, name="pair2_rounded")
         gather(4, 0, S)
-        nc.vector.tensor_copy(rounded[:], planes[5][:])
-        nc.scalar.activation(pairs[2][:, 1, :], rounded[:].indirect(offs_sb[:]), ACT.Copy)
-        x_codes[0] = keep.tile([P, S], U32, name="x_codes0", tag="plane5", align_bytes=64)
+        nc.scalar.copy(rounded[:, : T // 2], planes[5][:, : T // 2])
+        nc.gpsimd.tensor_copy(rounded[:, T // 2 :], planes[5][:, T // 2 :])
+        for a, b in [(0, S // 2), (S // 2, S)]:
+            nc.scalar.activation(
+                pairs[2][:, 1, a:b], rounded[:].indirect(offs_sb[:, a // PER_COL : b // PER_COL]), ACT.Copy
+            )
+        x_codes[0] = keep.tile([P, S], U32, name="x_codes0", tag="plane4", align_bytes=64)
         quantize(first[:], 0, 0, S)
         product(e_bank, 1, 0, 0, S)
         product(h_bank, 2, 0, 0, S)
         for s in range(SLICES):
             product(y_banks[s], 0, 0, s * SLICE, (s + 1) * SLICE)
-        for dst, (a, b) in zip(second, spans):
-            weave(dst, 2, a, b)
+        weave(second[-1], 2, *spans[-1])
+        for dst, (a, b) in zip(second[:-1], spans[:-1]):
+            nc.gpsimd.tensor_copy(dst[:, :, 0:2], pairs[2][:, :, a:b].rearrange("p e n -> p n e"))
         gather(6, 0, S - SLICE)
         whole = second[SLICES - 1]
         last = offs_sb[:, (S - SLICE) // PER_COL :]

@@ -38,7 +38,6 @@ def tile_picked_gatedg_relu_e_kernel(
         cen_sb = keep.tile([P, V // PER_COL], U16, name="cen_sb")
         pos1_sb = keep.tile([P, V // PER_COL], U16, name="pos1_sb")
         pos2_sb = keep.tile([P, V // PER_COL], U16, name="pos2_sb")
-        nc.sync.dma_start(offs_sb[:], offs)
 
         planes = [
             keep.tile([P, T], F32, name="plane%d" % j, tag="plane%d" % j, align_bytes=64) for j in range(PASSES * PACK)
@@ -49,24 +48,26 @@ def tile_picked_gatedg_relu_e_kernel(
             rows = xT[g * K_PASS : (g + 1) * K_PASS, :].rearrange("(p j) t -> p j t", j=PACK)
             nc.sync.dma_start(planes[j][:], rows[:, j % PACK, :])
 
-        staged = keep.tile([16, 3, PASSES, N], U8, name="staged")
+        load_plane(0)
+        nc.sync.dma_start(offs_sb[:], offs)
         w_scales = keep.tile([P, 3, PASSES, N], U8, name="w_scales", align_bytes=64)
         shared = keep.tile([P, 192 + 2 * 320], U8, name="shared", align_bytes=64)
         w_codes = [shared[:, 192:].rearrange("p (g b) -> p g b", g=PASSES)[:, :, : 2 * N]]
         w_codes += [keep.tile([P, PASSES, 2 * N], U8, name="w_codes%d" % i, align_bytes=64)[:] for i in (1, 2)]
         nc.vector.memset(w_scales[:].bitcast(I32), 0)
 
-        load_plane(0)
+        load_plane(1)
+        load_plane(2)
         for i, scales in enumerate((w1_scales, w2_scales, w3_scales)):
-            nc.sync.dma_start(staged[:, i, :, :].bitcast(I32), scales.rearrange("g r n -> r g n").bitcast(I32))
-        for j in range(1, 6):
+            nc.sync.dma_start(w_scales[0:16, i, :, :].bitcast(I32), scales.rearrange("g r n -> r g n").bitcast(I32))
+        for j in range(3, 6):
             load_plane(j)
-        for q in range(4):
+        load_plane(6)
+        for q in range(1, 4):
             nc.sync.dma_start(
                 w_scales[32 * q : 32 * q + 4].rearrange("r i g n -> r (i g n)").bitcast(I32),
-                staged[4 * q : 4 * q + 4].rearrange("r i g n -> r (i g n)").bitcast(I32),
+                w_scales[4 * q : 4 * q + 4].rearrange("r i g n -> r (i g n)").bitcast(I32),
             )
-        load_plane(6)
         for i in (1, 2, 0):
             words = (w1_words, w2_words, w3_words)[i]
             nc.sync.dma_start(w_codes[i].bitcast(I32), words.rearrange("g p b -> p g b").bitcast(I32))
@@ -119,9 +120,11 @@ def tile_picked_gatedg_relu_e_kernel(
         gather(1, 0, S)
         weave(first, 0, 0, S)
         gather(2, 0, S)
-        gather(3, 0, S)
-        weave(first[:, :320, :], 1, 0, 320)
-        nc.gpsimd.tensor_copy(first[:, 320:, 2:4], pairs[1][:, :, 320:].rearrange("p e n -> p n e"))
+        gather(3, 0, S // 2)
+        weave(first[:, : S // 2, :], 1, 0, S // 2)
+        gather(3, S // 2, S)
+        weave(first[:, S // 2 : S - SLICE, :], 1, S // 2, S - SLICE)
+        nc.gpsimd.tensor_copy(first[:, S - SLICE :, 2:4], pairs[1][:, :, S - SLICE :].rearrange("p e n -> p n e"))
 
         spans = [(s * SLICE, (s + 1) * SLICE) for s in range(SLICES)]
         second = [keep.tile([P, b - a, PACK], BF16, name="second%d" % a, align_bytes=64) for a, b in spans]
@@ -134,7 +137,7 @@ def tile_picked_gatedg_relu_e_kernel(
             nc.scalar.activation(
                 pairs[2][:, 1, a:b], rounded[:].indirect(offs_sb[:, a // PER_COL : b // PER_COL]), ACT.Copy
             )
-        x_codes[0] = keep.tile([P, S], U32, name="x_codes0", tag="plane4", align_bytes=64)
+        x_codes[0] = keep.tile([P, S], U32, name="x_codes0", align_bytes=64)
         quantize(first[:], 0, 0, S)
         product(e_bank, 1, 0, 0, S)
         product(h_bank, 2, 0, 0, S)

@@ -51,27 +51,25 @@ def tile_picked_gatedg_relu_e_kernel(
         load_plane(0)
         nc.sync.dma_start(offs_sb[:], offs)
         w_scales = keep.tile([P, 3, PASSES, N], U8, name="w_scales", align_bytes=64)
-        shared = keep.tile([P, 192 + 2 * 320], U8, name="shared", align_bytes=64)
-        w_codes = [shared[:, 192:].rearrange("p (g b) -> p g b", g=PASSES)[:, :, : 2 * N]]
-        w_codes += [keep.tile([P, PASSES, 2 * N], U8, name="w_codes%d" % i, align_bytes=64)[:] for i in (1, 2)]
+        shared = keep.tile([P, SLICE + 2 * 3 * SLICE], U8, name="shared", align_bytes=64)
+        w_codes = [keep.tile([P, PASSES, 2 * N], U8, name="w_codes%d" % i, align_bytes=64)[:] for i in (0, 2)]
+        w_codes.insert(1, shared[:, SLICE:].rearrange("p (g b) -> p g b", g=PASSES)[:, :, : 2 * N])
         nc.vector.memset(w_scales[:].bitcast(I32), 0)
 
         load_plane(1)
         load_plane(2)
         for i, scales in enumerate((w1_scales, w2_scales, w3_scales)):
             nc.sync.dma_start(w_scales[0:16, i, :, :].bitcast(I32), scales.rearrange("g r n -> r g n").bitcast(I32))
-        for j in range(3, 6):
+        for j in range(3, 7):
             load_plane(j)
-        load_plane(6)
         for q in range(1, 4):
             nc.sync.dma_start(
                 w_scales[32 * q : 32 * q + 4].rearrange("r i g n -> r (i g n)").bitcast(I32),
                 w_scales[4 * q : 4 * q + 4].rearrange("r i g n -> r (i g n)").bitcast(I32),
             )
-        for i in (1, 2, 0):
-            words = (w1_words, w2_words, w3_words)[i]
+        for i, words in enumerate((w1_words, w2_words, w3_words)):
             nc.sync.dma_start(w_codes[i].bitcast(I32), words.rearrange("g p b -> p g b").bitcast(I32))
-            if i == 1:
+            if i == 0:
                 load_plane(7)
         nc.sync.dma_start(cen_sb[:], cen)
         nc.sync.dma_start(pos1_sb[:], pos1)
@@ -82,20 +80,22 @@ def tile_picked_gatedg_relu_e_kernel(
         nc.vector.memset(warm_in[:], 0.0)
         nc.scalar.activation(warm_out[:], warm_in[:], ACT.Sigmoid)
 
-        x_codes = [None, keep.tile([P, S], U32, name="x_codes1", align_bytes=64)]
+        x_codes = [keep.tile([P, S], U32, name="x_codes%d" % g, align_bytes=64) for g in range(PASSES)]
         x_scales = [keep.tile([P, S], U8, name="x_scales0", align_bytes=64)[:], shared[:, :S]]
-        pairs = {u: keep.tile([P, 2, S], F32, name="pair%d" % u) for u in (0, 1, 3)}
-        y_banks = [psum.tile([P, SLICE], F32, name="y_bank%d" % s) for s in range(SLICES)]
-        e_bank = psum.tile([P, S], F32, name="e_bank")
-        h_bank = psum.tile([P, S], F32, name="h_bank")
+        pairs = [keep.tile([P, 2, S], BF16, name="pair%d" % u, align_bytes=64) for u in range(3)]
+        banks = [[psum.tile([P, S // 2], F32, name="bank%d_%d" % (i, c)) for c in range(2)] for i in range(3)]
 
-        def gather(j, a, b):
-            nc.vector.tensor_copy(
-                pairs[j // 2][:, j % 2, a:b], planes[j][:].indirect(offs_sb[:, a // PER_COL : b // PER_COL])
-            )
+        def picked(j, a, b):
+            return planes[j][:].indirect(offs_sb[:, a // PER_COL : b // PER_COL])
 
-        def weave(dst, u, a, b):
-            nc.scalar.copy(dst[:, :, 2 * (u % 2) : 2 * (u % 2) + 2], pairs[u][:, :, a:b].rearrange("p e n -> p n e"))
+        def gather_v(j, a, b):
+            nc.vector.tensor_copy(pairs[j // 2][:, j % 2, a:b], picked(j, a, b))
+
+        def gather_s(j, a, b):
+            nc.scalar.activation(pairs[j // 2][:, j % 2, a:b], picked(j, a, b), ACT.Copy)
+
+        def weave(copy, dst, u, a, b):
+            copy(dst[:, :, 2 * (u % 2) : 2 * (u % 2) + 2], pairs[u][:, :, a:b].rearrange("p e n -> p n e"))
 
         def quantize(src, g, a, b):
             nc.vector.quantize_mx(
@@ -104,9 +104,10 @@ def tile_picked_gatedg_relu_e_kernel(
                 in_=src.rearrange("p n t -> p (n t)"),
             )
 
-        def product(bank, i, g, a, b):
+        def product(i, c, g):
+            a, b = c * S // 2, (c + 1) * S // 2
             nc.tensor.matmul_mx(
-                out=bank[:],
+                out=banks[i][c][:],
                 lhsT=w_codes[i][:, g, :].bitcast(FP4X4),
                 lhsT_scale=w_scales[:, i, g, :],
                 rhs=x_codes[g][:, a:b].bitcast(FP8X4),
@@ -116,87 +117,72 @@ def tile_picked_gatedg_relu_e_kernel(
             )
 
         first = keep.tile([P, S, PACK], BF16, name="first", align_bytes=64)
-        gather(0, 0, S)
-        gather(1, 0, S)
-        weave(first, 0, 0, S)
-        gather(2, 0, S)
-        gather(3, 0, S // 2)
-        weave(first[:, : S // 2, :], 1, 0, S // 2)
-        gather(3, S // 2, S)
-        weave(first[:, S // 2 : S - SLICE, :], 1, S // 2, S - SLICE)
-        nc.gpsimd.tensor_copy(first[:, S - SLICE :, 2:4], pairs[1][:, :, S - SLICE :].rearrange("p e n -> p n e"))
+        for j in range(PACK):
+            gather_v(j, 0, S // 2)
+            gather_s(j, S // 2, S)
+            if j % 2 == 1:
+                weave(nc.vector.tensor_copy, first, j // 2, 0, S)
+        quantize(first[:], 0, 0, S)
+        for i in range(3):
+            for c in range(2):
+                product(i, c, 0)
 
         spans = [(s * SLICE, (s + 1) * SLICE) for s in range(SLICES)]
-        second = [keep.tile([P, b - a, PACK], BF16, name="second%d" % a, align_bytes=64) for a, b in spans]
-        rounded = keep.tile([P, T], BF16, name="rounded", align_bytes=64)
-        pairs[2] = keep.tile([P, 2, S], BF16, name="pair2_rounded")
-        gather(4, 0, S)
-        nc.scalar.copy(rounded[:, : T // 2], planes[5][:, : T // 2])
-        nc.gpsimd.tensor_copy(rounded[:, T // 2 :], planes[5][:, T // 2 :])
-        for a, b in [(0, S // 2), (S // 2, S)]:
-            nc.scalar.activation(
-                pairs[2][:, 1, a:b], rounded[:].indirect(offs_sb[:, a // PER_COL : b // PER_COL]), ACT.Copy
-            )
-        x_codes[0] = keep.tile([P, S], U32, name="x_codes0", align_bytes=64)
-        quantize(first[:], 0, 0, S)
-        product(e_bank, 1, 0, 0, S)
-        product(h_bank, 2, 0, 0, S)
+        parts = [keep.tile([P, SLICE, PACK], BF16, name="second%d" % s, align_bytes=64) for s in range(SLICES)]
+        late = {s: keep.tile([P, 2, SLICE], BF16, name="late%d" % s, align_bytes=64) for s in (2, 3)}
+        gather_s(4, 0, S)
+        gather_v(5, 0, S // 2)
+        gather_s(5, S // 2, S)
+        for s in (0, 1, 3):
+            weave(nc.vector.tensor_copy, parts[s], 2, *spans[s])
+        weave(nc.scalar.copy, parts[2], 2, *spans[2])
+        for j in (6, 7):
+            for s in (0, 1):
+                nc.vector.tensor_copy(parts[s][:, :, j - PACK], picked(j, *spans[s]))
+                nc.scalar.activation(late[s + 2][:, j % 2, :], picked(j, *spans[s + 2]), ACT.Copy)
+        nc.gpsimd.tensor_copy(parts[2][:, :, 2:4], late[2][:].rearrange("p e n -> p n e"))
+        nc.scalar.copy(parts[3][:, :, 2:4], late[3][:].rearrange("p e n -> p n e"))
         for s in range(SLICES):
-            product(y_banks[s], 0, 0, s * SLICE, (s + 1) * SLICE)
-        weave(second[-1], 2, *spans[-1])
-        for dst, (a, b) in zip(second[:-1], spans[:-1]):
-            nc.gpsimd.tensor_copy(dst[:, :, 0:2], pairs[2][:, :, a:b].rearrange("p e n -> p n e"))
-        gather(6, 0, S - SLICE)
-        whole = second[SLICES - 1]
-        last = offs_sb[:, (S - SLICE) // PER_COL :]
-        nc.vector.tensor_copy(whole[:, :, 2], planes[6][:].indirect(last))
-        for dst, (a, b) in zip(second[:-1], spans[:-1]):
-            gather(7, a, b)
-            weave(dst, 3, a, b)
-        nc.vector.tensor_copy(whole[:, :, 3], planes[7][:].indirect(last))
-        for s in (0, 3, 1, 2):
-            quantize(second[s][:], 1, *spans[s])
-            product(y_banks[s], 0, 1, *spans[s])
-        product(e_bank, 1, 1, 0, S)
-        product(h_bank, 2, 1, 0, S)
+            quantize(parts[s][:], 1, *spans[s])
+            if s % 2 == 1:
+                for i in range(3):
+                    product(i, s // 2, 1)
 
         y_sb = keep.tile([P, S], F32, name="y_sb")
         e_sb = keep.tile([P, S], F32, name="e_sb")
         h_sb = keep.tile([P, S], F32, name="h_sb")
-        for s in (0, 3, 1, 2):
-            nc.scalar.copy(y_sb[:, s * SLICE : (s + 1) * SLICE], y_banks[s][:])
-        nc.scalar.copy(e_sb[:], e_bank[:])
-        nc.scalar.copy(h_sb[:], h_bank[:])
+        nc.scalar.copy(y_sb[:, : S // 2], banks[0][0][:])
+        nc.vector.tensor_copy(e_sb[:, : S // 2], banks[1][0][:])
+        nc.scalar.copy(h_sb[:, : S // 2], banks[2][0][:])
+        nc.scalar.copy(y_sb[:, S // 2 :], banks[0][1][:])
+        nc.vector.tensor_copy(e_sb[:, S // 2 :], banks[1][1][:])
+        nc.vector.tensor_copy(h_sb[:, S // 2 :], banks[2][1][:])
 
         yc = keep.tile([P, V], F32, name="yc")
-        halves = [(0, HALF), (HALF, V)]
-        for a, b in halves:
-            nc.vector.tensor_copy(yc[:, a:b], y_sb[:].indirect(cen_sb[:, a // PER_COL : b // PER_COL]))
-        gates = []
-        for d, pos in enumerate((pos1_sb, pos2_sb)):
-            both = keep.tile([P, V], F32, name="both%d" % d)
-            gate = keep.tile([P, V], F32, name="gate%d" % d)
-            for a, b in halves if d == 0 else [(0, V)]:
-                nc.vector.tensor_tensor(
-                    both[:, a:b], e_sb[:].indirect(pos[:, a // PER_COL : b // PER_COL]), yc[:, a:b], ALU.add
-                )
-            nc.scalar.activation(gate[:], both[:], ACT.Sigmoid)
-            gates.append(gate)
-        passed1 = keep.tile([P, V], F32, name="passed1")
-        nc.vector.tensor_tensor(passed1[:], h_sb[:].indirect(pos1_sb[:]), gates[0][:], ALU.mult)
-        passed2 = [keep.tile([P, HALF], F32, name="passed2_%d" % c) for c in range(2)]
+        e1 = keep.tile([P, V], F32, name="e1")
+        both = [keep.tile([P, V], F32, name="both%d" % d) for d in range(2)]
+        gate = [keep.tile([P, V], F32, name="gate%d" % d) for d in range(2)]
+        hp = [keep.tile([P, V], F32, name="hp%d" % d) for d in range(2)]
+        passed = [keep.tile([P, V], F32, name="passed%d" % d) for d in range(2)]
+        halves = [slice(c * HALF, (c + 1) * HALF) for c in range(2)]
+        cols16 = [slice(c * HALF // PER_COL, (c + 1) * HALF // PER_COL) for c in range(2)]
+        nc.scalar.activation(yc[:], y_sb[:].indirect(cen_sb[:]), ACT.Copy)
+        nc.vector.tensor_copy(e1[:], e_sb[:].indirect(pos1_sb[:]))
+        nc.vector.tensor_tensor(both[1][:], e_sb[:].indirect(pos2_sb[:]), yc[:], ALU.add)
+        nc.vector.tensor_tensor(both[0][:], e1[:], yc[:], ALU.add)
+        nc.scalar.activation(hp[0][:], h_sb[:].indirect(pos1_sb[:]), ACT.Copy)
+        nc.scalar.activation(hp[1][:, halves[0]], h_sb[:].indirect(pos2_sb[:, cols16[0]]), ACT.Copy)
+        nc.vector.tensor_copy(hp[1][:, halves[1]], h_sb[:].indirect(pos2_sb[:, cols16[1]]))
+        nc.scalar.activation(gate[1][:], both[1][:], ACT.Sigmoid)
+        nc.vector.tensor_tensor(passed[1][:], hp[1][:], gate[1][:], ALU.mult)
         total = [keep.tile([P, HALF], F32, name="total%d" % c) for c in range(2)]
         result = [keep.tile([P, HALF], F32, name="result%d" % c) for c in range(2)]
-        for c in range(2):
-            cols = slice(c * HALF, (c + 1) * HALF)
-            nc.vector.tensor_tensor(
-                passed2[c][:],
-                h_sb[:].indirect(pos2_sb[:, c * HALF // PER_COL : (c + 1) * HALF // PER_COL]),
-                gates[1][:, cols],
-                ALU.mult,
-            )
-        for c in range(2):
-            nc.vector.tensor_tensor(total[c][:], passed1[:, c * HALF : (c + 1) * HALF], passed2[c][:], ALU.add)
-        for c in range(2):
+        for cols in halves:
+            nc.scalar.activation(gate[0][:, cols], both[0][:, cols], ACT.Sigmoid)
+        for cols in halves:
+            nc.vector.tensor_tensor(passed[0][:, cols], hp[0][:, cols], gate[0][:, cols], ALU.mult)
+        for c, cols in enumerate(halves):
+            nc.vector.tensor_tensor(total[c][:], passed[0][:, cols], passed[1][:, cols], ALU.add)
+        for c, cols in enumerate(halves):
             nc.vector.tensor_scalar_max(result[c][:], total[c][:], 0.0)
-            nc.sync.dma_start(out[:, c * HALF : (c + 1) * HALF], result[c][:])
+            nc.sync.dma_start(out[:, cols], result[c][:])

@@ -51,9 +51,9 @@ def tile_picked_gatedg_relu_e_kernel(
         load_plane(0)
         nc.sync.dma_start(offs_sb[:], offs)
         w_scales = keep.tile([P, 3, PASSES, N], U8, name="w_scales", align_bytes=64)
-        shared = keep.tile([P, SLICE + 2 * 3 * SLICE], U8, name="shared", align_bytes=64)
+        shared = keep.tile([P, 192 + 2 * 320], U8, name="shared", align_bytes=64)
         w_codes = [keep.tile([P, PASSES, 2 * N], U8, name="w_codes%d" % i, align_bytes=64)[:] for i in (0, 2)]
-        w_codes.insert(1, shared[:, SLICE:].rearrange("p (g b) -> p g b", g=PASSES)[:, :, : 2 * N])
+        w_codes.insert(1, shared[:, 192:].rearrange("p (g b) -> p g b", g=PASSES)[:, :, : 2 * N])
         nc.vector.memset(w_scales[:].bitcast(I32), 0)
 
         load_plane(1)
@@ -81,9 +81,15 @@ def tile_picked_gatedg_relu_e_kernel(
         nc.scalar.activation(warm_out[:], warm_in[:], ACT.Sigmoid)
 
         x_codes = [keep.tile([P, S], U32, name="x_codes%d" % g, align_bytes=64) for g in range(PASSES)]
-        x_scales = [keep.tile([P, S], U8, name="x_scales0", align_bytes=64)[:], shared[:, :S]]
+        first_scales = keep.tile([P, S], U8, name="first_scales", align_bytes=64)
+
+        def x_scales(g, a, b):
+            return (first_scales, shared)[g][:, a:b]
+
         pairs = [keep.tile([P, 2, S], BF16, name="pair%d" % u, align_bytes=64) for u in range(3)]
-        banks = [[psum.tile([P, S // 2], F32, name="bank%d_%d" % (i, c)) for c in range(2)] for i in range(3)]
+        pieces = [(0, S // 2), (S // 2, S - SLICE), (S - SLICE, S)]
+        cuts = [pieces, pieces, [(0, S)]]
+        banks = [[psum.tile([P, b - a], F32, name="bank%d_%d" % (i, a)) for a, b in cuts[i]] for i in range(3)]
 
         def picked(j, a, b):
             return planes[j][:].indirect(offs_sb[:, a // PER_COL : b // PER_COL])
@@ -100,18 +106,18 @@ def tile_picked_gatedg_relu_e_kernel(
         def quantize(src, g, a, b):
             nc.vector.quantize_mx(
                 out=x_codes[g][:, a:b].bitcast(FP8X4),
-                scales=x_scales[g][:, a:b],
+                scales=x_scales(g, a, b),
                 in_=src.rearrange("p n t -> p (n t)"),
             )
 
         def product(i, c, g):
-            a, b = c * S // 2, (c + 1) * S // 2
+            a, b = cuts[i][c]
             nc.tensor.matmul_mx(
                 out=banks[i][c][:],
                 lhsT=w_codes[i][:, g, :].bitcast(FP4X4),
                 lhsT_scale=w_scales[:, i, g, :],
                 rhs=x_codes[g][:, a:b].bitcast(FP8X4),
-                rhs_scale=x_scales[g][:, a:b],
+                rhs_scale=x_scales(g, a, b),
                 start=(g == 0),
                 stop=(g == PASSES - 1),
             )
@@ -124,65 +130,70 @@ def tile_picked_gatedg_relu_e_kernel(
                 weave(nc.vector.tensor_copy, first, j // 2, 0, S)
         quantize(first[:], 0, 0, S)
         for i in range(3):
-            for c in range(2):
+            for c in range(len(cuts[i])):
                 product(i, c, 0)
 
         spans = [(s * SLICE, (s + 1) * SLICE) for s in range(SLICES)]
         parts = [keep.tile([P, SLICE, PACK], BF16, name="second%d" % s, align_bytes=64) for s in range(SLICES)]
         late = {s: keep.tile([P, 2, SLICE], BF16, name="late%d" % s, align_bytes=64) for s in (2, 3)}
         gather_s(4, 0, S)
-        gather_v(5, 0, S // 2)
-        gather_s(5, S // 2, S)
-        for s in (0, 1, 3):
+        gather_s(5, 0, S)
+        for s in range(SLICES):
             weave(nc.vector.tensor_copy, parts[s], 2, *spans[s])
-        weave(nc.scalar.copy, parts[2], 2, *spans[2])
         for j in (6, 7):
             for s in (0, 1):
                 nc.vector.tensor_copy(parts[s][:, :, j - PACK], picked(j, *spans[s]))
                 nc.scalar.activation(late[s + 2][:, j % 2, :], picked(j, *spans[s + 2]), ACT.Copy)
-        nc.gpsimd.tensor_copy(parts[2][:, :, 2:4], late[2][:].rearrange("p e n -> p n e"))
+        nc.vector.tensor_copy(parts[2][:, :, 2:4], late[2][:].rearrange("p e n -> p n e"))
         nc.scalar.copy(parts[3][:, :, 2:4], late[3][:].rearrange("p e n -> p n e"))
         for s in range(SLICES):
             quantize(parts[s][:], 1, *spans[s])
-            if s % 2 == 1:
-                for i in range(3):
-                    product(i, s // 2, 1)
+        for c in range(len(pieces)):
+            for i in range(2):
+                product(i, c, 1)
+        product(2, 0, 1)
 
         y_sb = keep.tile([P, S], F32, name="y_sb")
         e_sb = keep.tile([P, S], F32, name="e_sb")
         h_sb = keep.tile([P, S], F32, name="h_sb")
-        nc.scalar.copy(y_sb[:, : S // 2], banks[0][0][:])
-        nc.vector.tensor_copy(e_sb[:, : S // 2], banks[1][0][:])
-        nc.scalar.copy(h_sb[:, : S // 2], banks[2][0][:])
-        nc.scalar.copy(y_sb[:, S // 2 :], banks[0][1][:])
-        nc.vector.tensor_copy(e_sb[:, S // 2 :], banks[1][1][:])
-        nc.vector.tensor_copy(h_sb[:, S // 2 :], banks[2][1][:])
+        for c, (a, b) in enumerate(pieces):
+            nc.scalar.copy(y_sb[:, a:b], banks[0][c][:])
+            nc.vector.tensor_copy(e_sb[:, a:b], banks[1][c][:])
+        nc.vector.tensor_copy(h_sb[:], banks[2][0][:])
 
-        yc = keep.tile([P, V], F32, name="yc")
-        e1 = keep.tile([P, V], F32, name="e1")
-        both = [keep.tile([P, V], F32, name="both%d" % d) for d in range(2)]
-        gate = [keep.tile([P, V], F32, name="gate%d" % d) for d in range(2)]
-        hp = [keep.tile([P, V], F32, name="hp%d" % d) for d in range(2)]
-        passed = [keep.tile([P, V], F32, name="passed%d" % d) for d in range(2)]
         halves = [slice(c * HALF, (c + 1) * HALF) for c in range(2)]
         cols16 = [slice(c * HALF // PER_COL, (c + 1) * HALF // PER_COL) for c in range(2)]
-        nc.scalar.activation(yc[:], y_sb[:].indirect(cen_sb[:]), ACT.Copy)
-        nc.vector.tensor_copy(e1[:], e_sb[:].indirect(pos1_sb[:]))
-        nc.vector.tensor_tensor(both[1][:], e_sb[:].indirect(pos2_sb[:]), yc[:], ALU.add)
-        nc.vector.tensor_tensor(both[0][:], e1[:], yc[:], ALU.add)
-        nc.scalar.activation(hp[0][:], h_sb[:].indirect(pos1_sb[:]), ACT.Copy)
-        nc.scalar.activation(hp[1][:, halves[0]], h_sb[:].indirect(pos2_sb[:, cols16[0]]), ACT.Copy)
-        nc.vector.tensor_copy(hp[1][:, halves[1]], h_sb[:].indirect(pos2_sb[:, cols16[1]]))
-        nc.scalar.activation(gate[1][:], both[1][:], ACT.Sigmoid)
-        nc.vector.tensor_tensor(passed[1][:], hp[1][:], gate[1][:], ALU.mult)
+        lists = (pos1_sb, pos2_sb)
+        yc = [keep.tile([P, HALF], F32, name="yc%d" % c) for c in range(2)]
+        both = [[keep.tile([P, HALF], F32, name="both%d_%d" % (c, d)) for d in range(2)] for c in range(2)]
+        gate = [[keep.tile([P, HALF], F32, name="gate%d_%d" % (c, d)) for d in range(2)] for c in range(2)]
+        passed = [[keep.tile([P, HALF], F32, name="passed%d_%d" % (c, d)) for d in range(2)] for c in range(2)]
         total = [keep.tile([P, HALF], F32, name="total%d" % c) for c in range(2)]
         result = [keep.tile([P, HALF], F32, name="result%d" % c) for c in range(2)]
-        for cols in halves:
-            nc.scalar.activation(gate[0][:, cols], both[0][:, cols], ACT.Sigmoid)
-        for cols in halves:
-            nc.vector.tensor_tensor(passed[0][:, cols], hp[0][:, cols], gate[0][:, cols], ALU.mult)
-        for c, cols in enumerate(halves):
-            nc.vector.tensor_tensor(total[c][:], passed[0][:, cols], passed[1][:, cols], ALU.add)
-        for c, cols in enumerate(halves):
+        h1 = keep.tile([P, V], F32, name="h1")
+        h2 = keep.tile([P, HALF], F32, name="h2")
+        for c in range(2):
+            nc.scalar.activation(yc[c][:], y_sb[:].indirect(cen_sb[:, cols16[c]]), ACT.Copy)
+        nc.scalar.activation(h1[:], h_sb[:].indirect(pos1_sb[:]), ACT.Copy)
+        for c in range(2):
+            for d in range(2):
+                nc.vector.tensor_tensor(both[c][d][:], e_sb[:].indirect(lists[d][:, cols16[c]]), yc[c][:], ALU.add)
+                nc.scalar.activation(gate[c][d][:], both[c][d][:], ACT.Sigmoid)
+            if c == 0:
+                nc.scalar.activation(h2[:], h_sb[:].indirect(pos2_sb[:, cols16[0]]), ACT.Copy)
+
+        def add_up(c):
+            nc.vector.tensor_tensor(total[c][:], passed[c][0][:], passed[c][1][:], ALU.add)
+
+        def finish(c):
             nc.vector.tensor_scalar_max(result[c][:], total[c][:], 0.0)
-            nc.sync.dma_start(out[:, cols], result[c][:])
+            nc.sync.dma_start(out[:, halves[c]], result[c][:])
+
+        nc.vector.tensor_tensor(passed[0][0][:], h1[:, halves[0]], gate[0][0][:], ALU.mult)
+        nc.vector.tensor_tensor(passed[0][1][:], h2[:], gate[0][1][:], ALU.mult)
+        nc.vector.tensor_tensor(passed[1][0][:], h1[:, halves[1]], gate[1][0][:], ALU.mult)
+        add_up(0)
+        nc.vector.tensor_tensor(passed[1][1][:], h_sb[:].indirect(pos2_sb[:, cols16[1]]), gate[1][1][:], ALU.mult)
+        finish(0)
+        add_up(1)
+        finish(1)

@@ -86,7 +86,7 @@ def tile_picked_gatedg_relu_e_kernel(
         def x_scales(g, a, b):
             return (first_scales, shared)[g][:, a:b]
 
-        pairs = [keep.tile([P, 2, S], BF16, name="pair%d" % u, align_bytes=64) for u in range(3)]
+        pairs = [keep.tile([P, 2, S], F32, name="pair%d" % u, align_bytes=64) for u in range(3)]
         pieces = [(0, S // 2), (S // 2, S - SLICE), (S - SLICE, S)]
         cuts = [pieces, pieces, [(0, S)]]
         banks = [[psum.tile([P, b - a], F32, name="bank%d_%d" % (i, a)) for a, b in cuts[i]] for i in range(3)]
@@ -123,11 +123,16 @@ def tile_picked_gatedg_relu_e_kernel(
             )
 
         first = keep.tile([P, S, PACK], BF16, name="first", align_bytes=64)
-        for j in range(PACK):
-            gather_v(j, 0, S // 2)
-            gather_s(j, S // 2, S)
-            if j % 2 == 1:
-                weave(nc.vector.tensor_copy, first, j // 2, 0, S)
+        gather_v(0, 0, S)
+        gather_v(1, 0, S)
+        weave(nc.scalar.copy, first, 0, 0, S)
+        gather_v(2, 0, S)
+        gather_v(3, 0, S // 2)
+        weave(nc.scalar.copy, first[:, : S // 2, :], 1, 0, S // 2)
+        gather_v(3, S // 2, S)
+        weave(nc.scalar.copy, first[:, S // 2 : S - SLICE, :], 1, S // 2, S - SLICE)
+        weave(nc.gpsimd.tensor_copy, first[:, S - SLICE :, :], 1, S - SLICE, S)
+        gather_v(4, 0, S)
         quantize(first[:], 0, 0, S)
         for i in range(3):
             for c in range(len(cuts[i])):
@@ -135,11 +140,11 @@ def tile_picked_gatedg_relu_e_kernel(
 
         spans = [(s * SLICE, (s + 1) * SLICE) for s in range(SLICES)]
         parts = [keep.tile([P, SLICE, PACK], BF16, name="second%d" % s, align_bytes=64) for s in range(SLICES)]
-        late = {s: keep.tile([P, 2, SLICE], BF16, name="late%d" % s, align_bytes=64) for s in (2, 3)}
-        gather_s(4, 0, S)
+        late = {s: keep.tile([P, 2, SLICE], F32, name="late%d" % s, align_bytes=64) for s in (2, 3)}
         gather_s(5, 0, S)
-        for s in range(SLICES):
+        for s in range(SLICES - 1):
             weave(nc.vector.tensor_copy, parts[s], 2, *spans[s])
+        weave(nc.gpsimd.tensor_copy, parts[3], 2, *spans[3])
         for j in (6, 7):
             for s in (0, 1):
                 nc.vector.tensor_copy(parts[s][:, :, j - PACK], picked(j, *spans[s]))

@@ -124,7 +124,8 @@ def tile_picked_gatedg_relu_e_kernel(
 
         first = keep.tile([P, S, PACK], BF16, name="first", align_bytes=64)
         gather_v(0, 0, S)
-        gather_v(1, 0, S)
+        gather_v(1, 0, S // 2)
+        gather_s(1, S // 2, S)
         weave(nc.scalar.copy, first, 0, 0, S)
         gather_v(2, 0, S)
         gather_v(3, 0, S // 2)

@@ -88,7 +88,7 @@ def tile_picked_gatedg_relu_e_kernel(
 
         pairs = [keep.tile([P, 2, S], F32, name="pair%d" % u, align_bytes=64) for u in range(3)]
         pieces = [(0, S // 2), (S // 2, S - SLICE), (S - SLICE, S)]
-        cuts = [pieces, pieces, [(0, S)]]
+        cuts = [pieces, [(0, S)], [(0, S)]]
         banks = [[psum.tile([P, b - a], F32, name="bank%d_%d" % (i, a)) for a, b in cuts[i]] for i in range(3)]
 
         def picked(j, a, b):
@@ -154,18 +154,15 @@ def tile_picked_gatedg_relu_e_kernel(
         nc.scalar.copy(parts[3][:, :, 2:4], late[3][:].rearrange("p e n -> p n e"))
         for s in range(SLICES):
             quantize(parts[s][:], 1, *spans[s])
-        for c in range(len(pieces)):
-            for i in range(2):
+        for i in range(3):
+            for c in range(len(cuts[i])):
                 product(i, c, 1)
-        product(2, 0, 1)
 
-        y_sb = keep.tile([P, S], F32, name="y_sb")
+        y_sb = keep.tile([P, S], F32, name="y_sb", tag="y_then_h")
         e_sb = keep.tile([P, S], F32, name="e_sb")
-        h_sb = keep.tile([P, S], F32, name="h_sb")
         for c, (a, b) in enumerate(pieces):
-            nc.scalar.copy(y_sb[:, a:b], banks[0][c][:])
-            nc.vector.tensor_copy(e_sb[:, a:b], banks[1][c][:])
-        nc.vector.tensor_copy(h_sb[:], banks[2][0][:])
+            (nc.vector.tensor_copy if c == 0 else nc.scalar.copy)(y_sb[:, a:b], banks[0][c][:])
+        nc.vector.tensor_copy(e_sb[:], banks[1][0][:])
 
         halves = [slice(c * HALF, (c + 1) * HALF) for c in range(2)]
         cols16 = [slice(c * HALF // PER_COL, (c + 1) * HALF // PER_COL) for c in range(2)]
@@ -176,17 +173,16 @@ def tile_picked_gatedg_relu_e_kernel(
         passed = [[keep.tile([P, HALF], F32, name="passed%d_%d" % (c, d)) for d in range(2)] for c in range(2)]
         total = [keep.tile([P, HALF], F32, name="total%d" % c) for c in range(2)]
         result = [keep.tile([P, HALF], F32, name="result%d" % c) for c in range(2)]
-        h1 = keep.tile([P, V], F32, name="h1")
-        h2 = keep.tile([P, HALF], F32, name="h2")
         for c in range(2):
             nc.scalar.activation(yc[c][:], y_sb[:].indirect(cen_sb[:, cols16[c]]), ACT.Copy)
-        nc.scalar.activation(h1[:], h_sb[:].indirect(pos1_sb[:]), ACT.Copy)
+        h_sb = keep.tile([P, S], F32, name="h_sb", tag="y_then_h")
+        nc.scalar.copy(h_sb[:], banks[2][0][:])
         for c in range(2):
             for d in range(2):
                 nc.vector.tensor_tensor(both[c][d][:], e_sb[:].indirect(lists[d][:, cols16[c]]), yc[c][:], ALU.add)
                 nc.scalar.activation(gate[c][d][:], both[c][d][:], ACT.Sigmoid)
-            if c == 0:
-                nc.scalar.activation(h2[:], h_sb[:].indirect(pos2_sb[:, cols16[0]]), ACT.Copy)
+        late_h = keep.tile([P, HALF], F32, name="late_h")
+        nc.scalar.activation(late_h[:], h_sb[:].indirect(pos2_sb[:, cols16[1]]), ACT.Copy)
 
         def add_up(c):
             nc.vector.tensor_tensor(total[c][:], passed[c][0][:], passed[c][1][:], ALU.add)
@@ -195,11 +191,10 @@ def tile_picked_gatedg_relu_e_kernel(
             nc.vector.tensor_scalar_max(result[c][:], total[c][:], 0.0)
             nc.sync.dma_start(out[:, halves[c]], result[c][:])
 
-        nc.vector.tensor_tensor(passed[0][0][:], h1[:, halves[0]], gate[0][0][:], ALU.mult)
-        nc.vector.tensor_tensor(passed[0][1][:], h2[:], gate[0][1][:], ALU.mult)
-        nc.vector.tensor_tensor(passed[1][0][:], h1[:, halves[1]], gate[1][0][:], ALU.mult)
-        add_up(0)
-        nc.vector.tensor_tensor(passed[1][1][:], h_sb[:].indirect(pos2_sb[:, cols16[1]]), gate[1][1][:], ALU.mult)
-        finish(0)
-        add_up(1)
-        finish(1)
+        for c, d in ((0, 0), (0, 1), (1, 0)):
+            nc.vector.tensor_tensor(passed[c][d][:], h_sb[:].indirect(lists[d][:, cols16[c]]), gate[c][d][:], ALU.mult)
+        nc.vector.tensor_tensor(passed[1][1][:], late_h[:], gate[1][1][:], ALU.mult)
+        for c in range(2):
+            add_up(c)
+        for c in range(2):
+            finish(c)

@@ -51,26 +51,24 @@ def tile_picked_gatedg_relu_e_kernel(
         load_plane(0)
         nc.sync.dma_start(offs_sb[:], offs)
         w_scales = keep.tile([P, 3, PASSES, N], U8, name="w_scales", align_bytes=64)
-        shared = keep.tile([P, 192 + 2 * 320], U8, name="shared", align_bytes=64)
-        w_codes = [keep.tile([P, PASSES, 2 * N], U8, name="w_codes%d" % i, align_bytes=64)[:] for i in (0, 2)]
-        w_codes.insert(1, shared[:, 192:].rearrange("p (g b) -> p g b", g=PASSES)[:, :, : 2 * N])
+        shared = keep.tile([P, S - SLICE + PASSES * 2 * N], U8, name="shared", align_bytes=64)
+        w_codes = [keep.tile([P, PASSES, 2 * N], U8, name="w_codes%d" % i, align_bytes=64)[:] for i in (1, 2)]
+        w_codes.insert(0, shared[:, S - SLICE :].rearrange("p (g b) -> p g b", g=PASSES))
         nc.vector.memset(w_scales[:].bitcast(I32), 0)
 
         load_plane(1)
         load_plane(2)
         for i, scales in enumerate((w1_scales, w2_scales, w3_scales)):
             nc.sync.dma_start(w_scales[0:16, i, :, :].bitcast(I32), scales.rearrange("g r n -> r g n").bitcast(I32))
-        for j in range(3, 7):
+        for j in range(3, 8):
             load_plane(j)
         for q in range(1, 4):
             nc.sync.dma_start(
                 w_scales[32 * q : 32 * q + 4].rearrange("r i g n -> r (i g n)").bitcast(I32),
                 w_scales[4 * q : 4 * q + 4].rearrange("r i g n -> r (i g n)").bitcast(I32),
             )
-        for i, words in enumerate((w1_words, w2_words, w3_words)):
+        for i, words in ((1, w2_words), (0, w1_words), (2, w3_words)):
             nc.sync.dma_start(w_codes[i].bitcast(I32), words.rearrange("g p b -> p g b").bitcast(I32))
-            if i == 0:
-                load_plane(7)
         nc.sync.dma_start(cen_sb[:], cen)
         nc.sync.dma_start(pos1_sb[:], pos1)
         nc.sync.dma_start(pos2_sb[:], pos2)
@@ -89,7 +87,7 @@ def tile_picked_gatedg_relu_e_kernel(
         pairs = [keep.tile([P, 2, S], F32, name="pair%d" % u, align_bytes=64) for u in range(3)]
         pieces = [(0, S // 2), (S // 2, S - SLICE), (S - SLICE, S)]
         cuts = [pieces, [(0, S)], [(0, S)]]
-        banks = [[psum.tile([P, b - a], F32, name="bank%d_%d" % (i, a)) for a, b in cuts[i]] for i in range(3)]
+        banks = [[psum.tile([P, b - a], F32, name="bank%d_%d" % (i, a)) for a, b in cuts[i]] for i in range(2)]
 
         def picked(j, a, b):
             return planes[j][:].indirect(offs_sb[:, a // PER_COL : b // PER_COL])
@@ -126,25 +124,30 @@ def tile_picked_gatedg_relu_e_kernel(
         gather_v(0, 0, S)
         gather_v(1, 0, S // 2)
         gather_s(1, S // 2, S)
-        weave(nc.scalar.copy, first, 0, 0, S)
-        gather_v(2, 0, S)
+        weave(nc.scalar.copy, first[:, : S // 2, :], 0, 0, S // 2)
+        weave(nc.gpsimd.tensor_copy, first[:, S // 2 :, :], 0, S // 2, S)
+        gather_v(2, 0, S - SLICE)
+        gather_s(2, S - SLICE, S)
         gather_v(3, 0, S // 2)
-        weave(nc.scalar.copy, first[:, : S // 2, :], 1, 0, S // 2)
-        gather_v(3, S // 2, S)
-        weave(nc.scalar.copy, first[:, S // 2 : S - SLICE, :], 1, S // 2, S - SLICE)
+        gather_s(3, S // 2, S)
+        weave(nc.vector.tensor_copy, first[:, :SLICE, :], 1, 0, SLICE)
+        weave(nc.scalar.copy, first[:, SLICE : S - SLICE, :], 1, SLICE, S - SLICE)
         weave(nc.gpsimd.tensor_copy, first[:, S - SLICE :, :], 1, S - SLICE, S)
-        gather_v(4, 0, S)
+        gather_v(4, 0, S // 2)
+        gather_s(4, S // 2, S)
         quantize(first[:], 0, 0, S)
-        for i in range(3):
+        for i in (1, 0):
             for c in range(len(cuts[i])):
                 product(i, c, 0)
 
         spans = [(s * SLICE, (s + 1) * SLICE) for s in range(SLICES)]
         parts = [keep.tile([P, SLICE, PACK], BF16, name="second%d" % s, align_bytes=64) for s in range(SLICES)]
         late = {s: keep.tile([P, 2, SLICE], F32, name="late%d" % s, align_bytes=64) for s in (2, 3)}
-        gather_s(5, 0, S)
-        for s in range(SLICES - 1):
+        gather_v(5, 0, S // 2)
+        gather_s(5, S // 2, S)
+        for s in (0, 1):
             weave(nc.vector.tensor_copy, parts[s], 2, *spans[s])
+        weave(nc.scalar.copy, parts[2], 2, *spans[2])
         weave(nc.gpsimd.tensor_copy, parts[3], 2, *spans[3])
         for j in (6, 7):
             for s in (0, 1):
@@ -154,7 +157,7 @@ def tile_picked_gatedg_relu_e_kernel(
         nc.scalar.copy(parts[3][:, :, 2:4], late[3][:].rearrange("p e n -> p n e"))
         for s in range(SLICES):
             quantize(parts[s][:], 1, *spans[s])
-        for i in range(3):
+        for i in range(2):
             for c in range(len(cuts[i])):
                 product(i, c, 1)
 
@@ -163,6 +166,9 @@ def tile_picked_gatedg_relu_e_kernel(
         for c, (a, b) in enumerate(pieces):
             (nc.vector.tensor_copy if c == 0 else nc.scalar.copy)(y_sb[:, a:b], banks[0][c][:])
         nc.vector.tensor_copy(e_sb[:], banks[1][0][:])
+        banks.append([psum.tile([P, S], F32, name="bank0_%d" % pieces[2][0])])
+        for g in range(PASSES):
+            product(2, 0, g)
 
         halves = [slice(c * HALF, (c + 1) * HALF) for c in range(2)]
         cols16 = [slice(c * HALF // PER_COL, (c + 1) * HALF // PER_COL) for c in range(2)]

@@ -20,9 +20,8 @@ P = 128
 PACK = 4
 K_PASS = P * PACK
 PASSES = K // K_PASS
-SLICE = 128
-SLICES = S // SLICE
 PER_COL = 16
+Q = S // 4
 HALF = V // 2
 
 
@@ -39,36 +38,41 @@ def tile_picked_gatedg_relu_e_kernel(
         pos1_sb = keep.tile([P, V // PER_COL], U16, name="pos1_sb")
         pos2_sb = keep.tile([P, V // PER_COL], U16, name="pos2_sb")
 
-        planes = [
-            keep.tile([P, T], F32, name="plane%d" % j, tag="plane%d" % j, align_bytes=64) for j in range(PASSES * PACK)
+        opening = keep.tile([P, 2, T], F32, name="opening", align_bytes=64)
+        planes = [opening[:, j, :] for j in range(2)]
+        planes.extend(keep.tile([P, T], F32, name="plane%d" % j, align_bytes=64)[:] for j in range(2, PASSES * PACK))
+        w_scales = keep.tile([P, 3, PASSES, N], U8, name="w_scales", align_bytes=64)
+        w_codes = [
+            [keep.tile([P, 2 * N], U8, name="w%d_codes%d" % (i, g), align_bytes=64)[:] for g in range(PASSES)]
+            for i in range(3)
         ]
+        w_words = (w1_words, w2_words, w3_words)
+
+        def load_words(i, g):
+            nc.sync.dma_start(w_codes[i][g].bitcast(I32), w_words[i][g].bitcast(I32))
+
+        nc.vector.memset(w_scales[:].bitcast(I32), 0)
 
         def load_plane(j):
             g = j // PACK
             rows = xT[g * K_PASS : (g + 1) * K_PASS, :].rearrange("(p j) t -> p j t", j=PACK)
-            nc.sync.dma_start(planes[j][:], rows[:, j % PACK, :])
+            nc.sync.dma_start(planes[j], rows[:, j % PACK, :])
 
-        load_plane(0)
+        nc.sync.dma_start(opening[:], xT[:K_PASS, :].rearrange("(p j) t -> p j t", j=PACK)[:, :2, :])
         nc.sync.dma_start(offs_sb[:], offs)
-        w_scales = keep.tile([P, 3, PASSES, N], U8, name="w_scales", align_bytes=64)
-        shared = keep.tile([P, S - SLICE + PASSES * 2 * N], U8, name="shared", align_bytes=64)
-        w_codes = [keep.tile([P, PASSES, 2 * N], U8, name="w_codes%d" % i, align_bytes=64)[:] for i in (1, 2)]
-        w_codes.insert(0, shared[:, S - SLICE :].rearrange("p (g b) -> p g b", g=PASSES))
-        nc.vector.memset(w_scales[:].bitcast(I32), 0)
-
-        load_plane(1)
-        load_plane(2)
         for i, scales in enumerate((w1_scales, w2_scales, w3_scales)):
             nc.sync.dma_start(w_scales[0:16, i, :, :].bitcast(I32), scales.rearrange("g r n -> r g n").bitcast(I32))
-        for j in range(3, 8):
+        for j in range(2, 7):
             load_plane(j)
+        load_words(0, 0)
         for q in range(1, 4):
             nc.sync.dma_start(
                 w_scales[32 * q : 32 * q + 4].rearrange("r i g n -> r (i g n)").bitcast(I32),
                 w_scales[4 * q : 4 * q + 4].rearrange("r i g n -> r (i g n)").bitcast(I32),
             )
-        for i, words in ((1, w2_words), (0, w1_words), (2, w3_words)):
-            nc.sync.dma_start(w_codes[i].bitcast(I32), words.rearrange("g p b -> p g b").bitcast(I32))
+        load_plane(7)
+        for i, g in ((1, 0), (2, 0), (0, 1), (1, 1), (2, 1)):
+            load_words(i, g)
         nc.sync.dma_start(cen_sb[:], cen)
         nc.sync.dma_start(pos1_sb[:], pos1)
         nc.sync.dma_start(pos2_sb[:], pos2)
@@ -79,32 +83,32 @@ def tile_picked_gatedg_relu_e_kernel(
         nc.scalar.activation(warm_out[:], warm_in[:], ACT.Sigmoid)
 
         x_codes = [keep.tile([P, S], U32, name="x_codes%d" % g, align_bytes=64) for g in range(PASSES)]
-        first_scales = keep.tile([P, S], U8, name="first_scales", align_bytes=64)
+        x_scales = [keep.tile([P, S], U8, name="x_scales%d" % g, align_bytes=64) for g in range(PASSES)]
 
-        def x_scales(g, a, b):
-            return (first_scales, shared)[g][:, a:b]
+        near, far, third, last = (0, 2 * Q), (2 * Q, S), (2 * Q, 3 * Q), (3 * Q, S)
+        cuts = [[near, third, last], [near, far], [(0, S)]]
+        banks = [[psum.tile([P, b - a], F32, name="bank%d_%d" % (i, a)) for a, b in cuts[i]] for i in range(3)]
 
-        pairs = [keep.tile([P, 2, S], F32, name="pair%d" % u, align_bytes=64) for u in range(3)]
-        pieces = [(0, S // 2), (S // 2, S - SLICE), (S - SLICE, S)]
-        cuts = [pieces, [(0, S)], [(0, S)]]
-        banks = [[psum.tile([P, b - a], F32, name="bank%d_%d" % (i, a)) for a, b in cuts[i]] for i in range(2)]
+        def picked(j, span):
+            return planes[j].indirect(offs_sb[:, span[0] // PER_COL : span[1] // PER_COL])
 
-        def picked(j, a, b):
-            return planes[j][:].indirect(offs_sb[:, a // PER_COL : b // PER_COL])
+        def gather_v(dst, j, span):
+            nc.vector.tensor_copy(dst, picked(j, span))
 
-        def gather_v(j, a, b):
-            nc.vector.tensor_copy(pairs[j // 2][:, j % 2, a:b], picked(j, a, b))
+        def gather_s(dst, j, span):
+            nc.scalar.activation(dst, picked(j, span), ACT.Copy)
 
-        def gather_s(j, a, b):
-            nc.scalar.activation(pairs[j // 2][:, j % 2, a:b], picked(j, a, b), ACT.Copy)
+        def copy_g(dst, src):
+            nc.gpsimd.tensor_scalar(dst, src, 1.0, 0.0, ALU.mult, ALU.add)
 
-        def weave(copy, dst, u, a, b):
-            copy(dst[:, :, 2 * (u % 2) : 2 * (u % 2) + 2], pairs[u][:, :, a:b].rearrange("p e n -> p n e"))
+        def weave(copy, dst, u, src):
+            copy(dst[:, :, 2 * u : 2 * u + 2], src.rearrange("p e n -> p n e"))
 
-        def quantize(src, g, a, b):
+        def quantize(src, g, span):
+            a, b = span
             nc.vector.quantize_mx(
                 out=x_codes[g][:, a:b].bitcast(FP8X4),
-                scales=x_scales(g, a, b),
+                scales=x_scales[g][:, a:b],
                 in_=src.rearrange("p n t -> p (n t)"),
             )
 
@@ -112,63 +116,72 @@ def tile_picked_gatedg_relu_e_kernel(
             a, b = cuts[i][c]
             nc.tensor.matmul_mx(
                 out=banks[i][c][:],
-                lhsT=w_codes[i][:, g, :].bitcast(FP4X4),
+                lhsT=w_codes[i][g].bitcast(FP4X4),
                 lhsT_scale=w_scales[:, i, g, :],
                 rhs=x_codes[g][:, a:b].bitcast(FP8X4),
-                rhs_scale=x_scales(g, a, b),
+                rhs_scale=x_scales[g][:, a:b],
                 start=(g == 0),
                 stop=(g == PASSES - 1),
             )
 
         first = keep.tile([P, S, PACK], BF16, name="first", align_bytes=64)
-        gather_v(0, 0, S)
-        gather_v(1, 0, S // 2)
-        gather_s(1, S // 2, S)
-        weave(nc.scalar.copy, first[:, : S // 2, :], 0, 0, S // 2)
-        weave(nc.gpsimd.tensor_copy, first[:, S // 2 :, :], 0, S // 2, S)
-        gather_v(2, 0, S - SLICE)
-        gather_s(2, S - SLICE, S)
-        gather_v(3, 0, S // 2)
-        gather_s(3, S // 2, S)
-        weave(nc.vector.tensor_copy, first[:, :SLICE, :], 1, 0, SLICE)
-        weave(nc.scalar.copy, first[:, SLICE : S - SLICE, :], 1, SLICE, S - SLICE)
-        weave(nc.gpsimd.tensor_copy, first[:, S - SLICE :, :], 1, S - SLICE, S)
-        gather_v(4, 0, S // 2)
-        gather_s(4, S // 2, S)
-        quantize(first[:], 0, 0, S)
-        for i in (1, 0):
-            for c in range(len(cuts[i])):
-                product(i, c, 0)
+        trio = keep.tile([P, 3, 2 * Q], F32, name="trio", align_bytes=64)
+        low = keep.tile([P, 2, 2 * Q], F32, name="low", align_bytes=64)
+        high = [keep.tile([P, 2, Q], F32, name="high%d" % s, align_bytes=64) for s in range(2)]
+        for j in range(PACK):
+            if j < 3:
+                gather_v(trio[:, j, :], j, near)
+            else:
+                nc.vector.tensor_copy(first[:, : 2 * Q, :3], trio[:].rearrange("p e n -> p n e"))
+                gather_v(first[:, : 2 * Q, j], j, near)
+            if j < 2:
+                gather_s(low[:, j, :], j, far)
+            else:
+                for tile, span in zip(high, (third, last)):
+                    gather_s(tile[:, j % 2, :], j, span)
+            if j == 1:
+                weave(copy_g, first[:, 2 * Q :, :], 0, low[:])
+        for tile, (a, b) in zip(high, (third, last)):
+            weave(copy_g, first[:, a:b, :], 1, tile[:])
 
-        spans = [(s * SLICE, (s + 1) * SLICE) for s in range(SLICES)]
-        parts = [keep.tile([P, SLICE, PACK], BF16, name="second%d" % s, align_bytes=64) for s in range(SLICES)]
-        late = {s: keep.tile([P, 2, SLICE], F32, name="late%d" % s, align_bytes=64) for s in (2, 3)}
-        gather_v(5, 0, S // 2)
-        gather_s(5, S // 2, S)
-        for s in (0, 1):
-            weave(nc.vector.tensor_copy, parts[s], 2, *spans[s])
-        weave(nc.scalar.copy, parts[2], 2, *spans[2])
-        weave(nc.gpsimd.tensor_copy, parts[3], 2, *spans[3])
+        spans = [(s * Q, (s + 1) * Q) for s in range(4)]
+        parts = [keep.tile([P, Q, PACK], BF16, name="second%d" % s, align_bytes=64) for s in range(4)]
+        early = [keep.tile([P, 2, Q], F32, name="early%d" % s, align_bytes=64) for s in range(3)]
+        late = keep.tile([P, 2, Q], F32, name="late", align_bytes=64)
+        for j in (4, 5):
+            gather_v(early[0][:, j % 2, :], j, (Q, 2 * Q))
+            gather_v(parts[0][:, :, j - PACK], j, spans[0])
+            gather_s(early[1][:, j % 2, :], j, third)
+            gather_s(early[2][:, j % 2, :], j, last)
+            if j == 4:
+                quantize(first[:], 0, (0, S))
+                for i in range(3):
+                    for c in range(len(cuts[i])):
+                        product(i, c, 0)
+        weave(nc.scalar.copy, parts[1][:], 0, early[0][:])
+        weave(copy_g, parts[2][:], 0, early[1][:])
+        weave(copy_g, parts[3][:], 0, early[2][:])
         for j in (6, 7):
-            for s in (0, 1):
-                nc.vector.tensor_copy(parts[s][:, :, j - PACK], picked(j, *spans[s]))
-                nc.scalar.activation(late[s + 2][:, j % 2, :], picked(j, *spans[s + 2]), ACT.Copy)
-        nc.vector.tensor_copy(parts[2][:, :, 2:4], late[2][:].rearrange("p e n -> p n e"))
-        nc.scalar.copy(parts[3][:, :, 2:4], late[3][:].rearrange("p e n -> p n e"))
-        for s in range(SLICES):
-            quantize(parts[s][:], 1, *spans[s])
-        for i in range(2):
-            for c in range(len(cuts[i])):
-                product(i, c, 1)
+            for s in range(2):
+                gather_v(parts[s][:, :, j - PACK], j, spans[s])
+            if j == 6:
+                gather_s(late[:, 0, :], j, last)
+            gather_s(early[1][:, j % 2, :], j, third)
+            if j == 7:
+                gather_s(late[:, 1, :], j, last)
+        weave(nc.vector.tensor_copy, parts[2][:], 1, early[1][:])
+        weave(nc.scalar.copy, parts[3][:], 1, late[:])
+        for part, span in zip(parts, spans):
+            quantize(part[:], 1, span)
+        for i, c in ((0, 0), (0, 1), (0, 2), (1, 0), (1, 1), (2, 0)):
+            product(i, c, 1)
 
         y_sb = keep.tile([P, S], F32, name="y_sb", tag="y_then_h")
         e_sb = keep.tile([P, S], F32, name="e_sb")
-        for c, (a, b) in enumerate(pieces):
-            (nc.vector.tensor_copy if c == 0 else nc.scalar.copy)(y_sb[:, a:b], banks[0][c][:])
-        nc.vector.tensor_copy(e_sb[:], banks[1][0][:])
-        banks.append([psum.tile([P, S], F32, name="bank0_%d" % pieces[2][0])])
-        for g in range(PASSES):
-            product(2, 0, g)
+        for c, (a, b) in enumerate(cuts[0]):
+            nc.scalar.copy(y_sb[:, a:b], banks[0][c][:])
+        for c, (a, b) in enumerate(cuts[1]):
+            nc.vector.tensor_copy(e_sb[:, a:b], banks[1][c][:])
 
         halves = [slice(c * HALF, (c + 1) * HALF) for c in range(2)]
         cols16 = [slice(c * HALF // PER_COL, (c + 1) * HALF // PER_COL) for c in range(2)]
@@ -178,7 +191,7 @@ def tile_picked_gatedg_relu_e_kernel(
         gate = [[keep.tile([P, HALF], F32, name="gate%d_%d" % (c, d)) for d in range(2)] for c in range(2)]
         passed = [[keep.tile([P, HALF], F32, name="passed%d_%d" % (c, d)) for d in range(2)] for c in range(2)]
         total = [keep.tile([P, HALF], F32, name="total%d" % c) for c in range(2)]
-        result = [keep.tile([P, HALF], F32, name="result%d" % c) for c in range(2)]
+        result = keep.tile([P, V], F32, name="result")
         for c in range(2):
             nc.scalar.activation(yc[c][:], y_sb[:].indirect(cen_sb[:, cols16[c]]), ACT.Copy)
         h_sb = keep.tile([P, S], F32, name="h_sb", tag="y_then_h")
@@ -190,17 +203,11 @@ def tile_picked_gatedg_relu_e_kernel(
         late_h = keep.tile([P, HALF], F32, name="late_h")
         nc.scalar.activation(late_h[:], h_sb[:].indirect(pos2_sb[:, cols16[1]]), ACT.Copy)
 
-        def add_up(c):
-            nc.vector.tensor_tensor(total[c][:], passed[c][0][:], passed[c][1][:], ALU.add)
-
-        def finish(c):
-            nc.vector.tensor_scalar_max(result[c][:], total[c][:], 0.0)
-            nc.sync.dma_start(out[:, halves[c]], result[c][:])
-
         for c, d in ((0, 0), (0, 1), (1, 0)):
             nc.vector.tensor_tensor(passed[c][d][:], h_sb[:].indirect(lists[d][:, cols16[c]]), gate[c][d][:], ALU.mult)
         nc.vector.tensor_tensor(passed[1][1][:], late_h[:], gate[1][1][:], ALU.mult)
         for c in range(2):
-            add_up(c)
+            nc.vector.tensor_tensor(total[c][:], passed[c][0][:], passed[c][1][:], ALU.add)
         for c in range(2):
-            finish(c)
+            nc.vector.tensor_scalar_max(result[:, halves[c]], total[c][:], 0.0)
+        nc.sync.dma_start(out, result[:])

@@ -126,23 +126,19 @@ def tile_picked_gatedg_relu_e_kernel(
 
         first = keep.tile([P, S, PACK], BF16, name="first", align_bytes=64)
         trio = keep.tile([P, 3, 2 * Q], F32, name="trio", align_bytes=64)
-        low = keep.tile([P, 2, 2 * Q], F32, name="low", align_bytes=64)
-        high = [keep.tile([P, 2, Q], F32, name="high%d" % s, align_bytes=64) for s in range(2)]
         for j in range(PACK):
             if j < 3:
                 gather_v(trio[:, j, :], j, near)
             else:
                 nc.vector.tensor_copy(first[:, : 2 * Q, :3], trio[:].rearrange("p e n -> p n e"))
                 gather_v(first[:, : 2 * Q, j], j, near)
-            if j < 2:
-                gather_s(low[:, j, :], j, far)
-            else:
-                for tile, span in zip(high, (third, last)):
-                    gather_s(tile[:, j % 2, :], j, span)
-            if j == 1:
-                weave(copy_g, first[:, 2 * Q :, :], 0, low[:])
-        for tile, (a, b) in zip(high, (third, last)):
-            weave(copy_g, first[:, a:b, :], 1, tile[:])
+        for u in range(2):
+            tiles = [keep.tile([P, 2, Q], F32, name="pair%d_%d" % (u, s), align_bytes=64) for s in range(2)]
+            order = [(s, e) for s in range(2) for e in range(2)] if u == 0 else [(s, e) for e in range(2) for s in range(2)]
+            for s, e in order:
+                gather_s(tiles[s][:, e, :], 2 * u + e, (third, last)[s])
+            for tile, (a, b) in zip(tiles, (third, last)):
+                weave(copy_g, first[:, a:b, :], u, tile[:])
 
         spans = [(s * Q, (s + 1) * Q) for s in range(4)]
         parts = [keep.tile([P, Q, PACK], BF16, name="second%d" % s, align_bytes=64) for s in range(4)]
@@ -179,7 +175,7 @@ def tile_picked_gatedg_relu_e_kernel(
         y_sb = keep.tile([P, S], F32, name="y_sb", tag="y_then_h")
         e_sb = keep.tile([P, S], F32, name="e_sb")
         for c, (a, b) in enumerate(cuts[0]):
-            nc.scalar.copy(y_sb[:, a:b], banks[0][c][:])
+            (nc.vector.tensor_copy if c == 0 else nc.scalar.copy)(y_sb[:, a:b], banks[0][c][:])
         for c, (a, b) in enumerate(cuts[1]):
             nc.vector.tensor_copy(e_sb[:, a:b], banks[1][c][:])
 

@@ -42,9 +42,10 @@ def tile_picked_gatedg_relu_e_kernel(
         planes = [opening[:, j, :] for j in range(2)]
         planes.extend(keep.tile([P, T], F32, name="plane%d" % j, align_bytes=64)[:] for j in range(2, PASSES * PACK))
         w_scales = keep.tile([P, 3, PASSES, N], U8, name="w_scales", align_bytes=64)
+        second_words = keep.tile([P, 3, 2 * N], U8, name="second_words", align_bytes=64)
+        far_words = keep.tile([P, 3, 2 * N], U8, name="far_words", align_bytes=64)
         w_codes = [
-            [keep.tile([P, 2 * N], U8, name="w%d_codes%d" % (i, g), align_bytes=64)[:] for g in range(PASSES)]
-            for i in range(3)
+            [keep.tile([P, 2 * N], U8, name="w%d_codes" % i, align_bytes=64)[:], second_words[:, i, :]] for i in range(3)
         ]
         w_words = (w1_words, w2_words, w3_words)
 
@@ -86,8 +87,13 @@ def tile_picked_gatedg_relu_e_kernel(
         x_scales = [keep.tile([P, S], U8, name="x_scales%d" % g, align_bytes=64) for g in range(PASSES)]
 
         near, far, third, last = (0, 2 * Q), (2 * Q, S), (2 * Q, 3 * Q), (3 * Q, S)
-        cuts = [[near, third, last], [near, far], [(0, S)]]
-        banks = [[psum.tile([P, b - a], F32, name="bank%d_%d" % (i, a)) for a, b in cuts[i]] for i in range(3)]
+        one, two = (0, Q), (Q, 2 * Q)
+        cuts = [[one, two, third, last], [one, two, far], [one, two, far]]
+        joint = [psum.tile([P, 3, Q], F32, name="joint%d" % s) for s in range(2)]
+        banks = [
+            [joint[c][:, i, :] if c < 2 else psum.tile([P, b - a], F32, name="bank%d_%d" % (i, a))[:] for c, (a, b) in enumerate(cuts[i])]
+            for i in range(3)
+        ]
 
         def picked(j, span):
             return planes[j].indirect(offs_sb[:, span[0] // PER_COL : span[1] // PER_COL])
@@ -115,13 +121,13 @@ def tile_picked_gatedg_relu_e_kernel(
         def product(i, c, g):
             a, b = cuts[i][c]
             nc.tensor.matmul_mx(
-                out=banks[i][c][:],
-                lhsT=w_codes[i][g].bitcast(FP4X4),
+                out=banks[i][c],
+                lhsT=(far_words[:, i, :] if g == 1 and c >= 2 else w_codes[i][g]).bitcast(FP4X4),
                 lhsT_scale=w_scales[:, i, g, :],
                 rhs=x_codes[g][:, a:b].bitcast(FP8X4),
                 rhs_scale=x_scales[g][:, a:b],
-                start=(g == 0),
-                stop=(g == PASSES - 1),
+                start=(g == 0 and (c >= 2 or i == 0)),
+                stop=(g == PASSES - 1 and (c >= 2 or i == 0)),
             )
 
         first = keep.tile([P, S, PACK], BF16, name="first", align_bytes=64)
@@ -160,24 +166,40 @@ def tile_picked_gatedg_relu_e_kernel(
         for j in (6, 7):
             for s in range(2):
                 gather_v(parts[s][:, :, j - PACK], j, spans[s])
-            if j == 6:
-                gather_s(late[:, 0, :], j, last)
+            gather_s(late[:, j % 2, :], j, last)
             gather_s(early[1][:, j % 2, :], j, third)
-            if j == 7:
-                gather_s(late[:, 1, :], j, last)
-        weave(nc.vector.tensor_copy, parts[2][:], 1, early[1][:])
         weave(nc.scalar.copy, parts[3][:], 1, late[:])
-        for part, span in zip(parts, spans):
-            quantize(part[:], 1, span)
-        for i, c in ((0, 0), (0, 1), (0, 2), (1, 0), (1, 1), (2, 0)):
+        quantize(parts[0][:], 1, spans[0])
+        weave(nc.vector.tensor_copy, parts[2][:], 1, early[1][:])
+        for s in (1, 3, 2):
+            quantize(parts[s][:], 1, spans[s])
+        nc.scalar.copy(
+            far_words[:].rearrange("p i b -> p (i b)").bitcast(U32),
+            second_words[:].rearrange("p i b -> p (i b)").bitcast(U32),
+        )
+        for c in range(2):
+            for i in (2, 1, 0):
+                product(i, c, 1)
+        for i, c in ((0, 3), (0, 2), (1, 2), (2, 2)):
             product(i, c, 1)
 
-        y_sb = keep.tile([P, S], F32, name="y_sb", tag="y_then_h")
-        e_sb = keep.tile([P, S], F32, name="e_sb")
-        for c, (a, b) in enumerate(cuts[0]):
-            (nc.vector.tensor_copy if c == 0 else nc.scalar.copy)(y_sb[:, a:b], banks[0][c][:])
-        for c, (a, b) in enumerate(cuts[1]):
-            nc.vector.tensor_copy(e_sb[:, a:b], banks[1][c][:])
+        results = [keep.tile([P, S], F32, name=name) for name in ("y_sb", "e_sb", "h_sb")]
+        y_sb, e_sb, h_sb = results
+
+        def empty(copy, i, c):
+            a, b = cuts[i][c]
+            copy(results[i][:, a:b], banks[i][c])
+
+        for i in range(2):
+            empty(nc.scalar.copy, i, 0)
+        empty(nc.vector.tensor_copy, 2, 0)
+        for i in range(2):
+            empty(nc.vector.tensor_copy, i, 1)
+        for c in (3, 2):
+            empty(nc.scalar.copy, 0, c)
+        empty(nc.scalar.copy, 2, 1)
+        for i in (1, 2):
+            empty(nc.vector.tensor_copy, i, 2)
 
         halves = [slice(c * HALF, (c + 1) * HALF) for c in range(2)]
         cols16 = [slice(c * HALF // PER_COL, (c + 1) * HALF // PER_COL) for c in range(2)]
@@ -187,21 +209,22 @@ def tile_picked_gatedg_relu_e_kernel(
         gate = [[keep.tile([P, HALF], F32, name="gate%d_%d" % (c, d)) for d in range(2)] for c in range(2)]
         passed = [[keep.tile([P, HALF], F32, name="passed%d_%d" % (c, d)) for d in range(2)] for c in range(2)]
         total = [keep.tile([P, HALF], F32, name="total%d" % c) for c in range(2)]
+        h_pos2 = keep.tile([P, V], F32, name="h_pos2")
         result = keep.tile([P, V], F32, name="result")
         for c in range(2):
             nc.scalar.activation(yc[c][:], y_sb[:].indirect(cen_sb[:, cols16[c]]), ACT.Copy)
-        h_sb = keep.tile([P, S], F32, name="h_sb", tag="y_then_h")
-        nc.scalar.copy(h_sb[:], banks[2][0][:])
-        for c in range(2):
-            for d in range(2):
-                nc.vector.tensor_tensor(both[c][d][:], e_sb[:].indirect(lists[d][:, cols16[c]]), yc[c][:], ALU.add)
+        nc.scalar.activation(h_pos2[:], h_sb[:].indirect(pos2_sb[:]), ACT.Copy)
+        early_e = keep.tile([P, HALF], F32, name="early_e")
+        nc.vector.tensor_copy(early_e[:], e_sb[:].indirect(pos1_sb[:, cols16[1]]))
+        for d in range(2):
+            for c in range(2):
+                source = early_e[:] if (c, d) == (1, 0) else e_sb[:].indirect(lists[d][:, cols16[c]])
+                nc.vector.tensor_tensor(both[c][d][:], source, yc[c][:], ALU.add)
                 nc.scalar.activation(gate[c][d][:], both[c][d][:], ACT.Sigmoid)
-        late_h = keep.tile([P, HALF], F32, name="late_h")
-        nc.scalar.activation(late_h[:], h_sb[:].indirect(pos2_sb[:, cols16[1]]), ACT.Copy)
-
-        for c, d in ((0, 0), (0, 1), (1, 0)):
-            nc.vector.tensor_tensor(passed[c][d][:], h_sb[:].indirect(lists[d][:, cols16[c]]), gate[c][d][:], ALU.mult)
-        nc.vector.tensor_tensor(passed[1][1][:], late_h[:], gate[1][1][:], ALU.mult)
+        for c in range(2):
+            nc.vector.tensor_tensor(passed[c][0][:], h_sb[:].indirect(pos1_sb[:, cols16[c]]), gate[c][0][:], ALU.mult)
+        for c in range(2):
+            nc.vector.tensor_tensor(passed[c][1][:], h_pos2[:, halves[c]], gate[c][1][:], ALU.mult)
         for c in range(2):
             nc.vector.tensor_tensor(total[c][:], passed[c][0][:], passed[c][1][:], ALU.add)
         for c in range(2):

@@ -38,16 +38,15 @@ def tile_picked_gatedg_relu_e_kernel(
         pos1_sb = keep.tile([P, V // PER_COL], U16, name="pos1_sb")
         pos2_sb = keep.tile([P, V // PER_COL], U16, name="pos2_sb")
 
-        opening = keep.tile([P, 2, T], F32, name="opening", align_bytes=64)
-        planes = [opening[:, j, :] for j in range(2)]
-        planes.extend(keep.tile([P, T], F32, name="plane%d" % j, align_bytes=64)[:] for j in range(2, PASSES * PACK))
+        planes = [keep.tile([P, T], F32, name="plane%d" % j, align_bytes=64)[:] for j in range(PASSES * PACK)]
         w_scales = keep.tile([P, 3, PASSES, N], U8, name="w_scales", align_bytes=64)
-        second_words = keep.tile([P, 3, 2 * N], U8, name="second_words", align_bytes=64)
+        late_words = keep.tile([P, 4, 2 * N], U8, name="late_words", align_bytes=64)
         far_words = keep.tile([P, 3, 2 * N], U8, name="far_words", align_bytes=64)
         w_codes = [
-            [keep.tile([P, 2 * N], U8, name="w%d_codes" % i, align_bytes=64)[:], second_words[:, i, :]] for i in range(3)
+            [keep.tile([P, 2 * N], U8, name="w%d_codes" % i, align_bytes=64)[:], late_words[:, 2 + i, :]] for i in range(2)
         ]
-        w_words = (w1_words, w2_words, w3_words)
+        w_codes.append([late_words[:, g, :] for g in range(PASSES)])
+        w_words = (w1_words, w2_words)
 
         def load_words(i, g):
             nc.sync.dma_start(w_codes[i][g].bitcast(I32), w_words[i][g].bitcast(I32))
@@ -59,11 +58,11 @@ def tile_picked_gatedg_relu_e_kernel(
             rows = xT[g * K_PASS : (g + 1) * K_PASS, :].rearrange("(p j) t -> p j t", j=PACK)
             nc.sync.dma_start(planes[j], rows[:, j % PACK, :])
 
-        nc.sync.dma_start(opening[:], xT[:K_PASS, :].rearrange("(p j) t -> p j t", j=PACK)[:, :2, :])
+        load_plane(0)
         nc.sync.dma_start(offs_sb[:], offs)
         for i, scales in enumerate((w1_scales, w2_scales, w3_scales)):
             nc.sync.dma_start(w_scales[0:16, i, :, :].bitcast(I32), scales.rearrange("g r n -> r g n").bitcast(I32))
-        for j in range(2, 7):
+        for j in range(1, 7):
             load_plane(j)
         load_words(0, 0)
         for q in range(1, 4):
@@ -72,8 +71,10 @@ def tile_picked_gatedg_relu_e_kernel(
                 w_scales[4 * q : 4 * q + 4].rearrange("r i g n -> r (i g n)").bitcast(I32),
             )
         load_plane(7)
-        for i, g in ((1, 0), (2, 0), (0, 1), (1, 1), (2, 1)):
-            load_words(i, g)
+        load_words(1, 0)
+        nc.sync.dma_start(late_words[:, :2, :].bitcast(I32), w3_words.rearrange("g p b -> p g b").bitcast(I32))
+        for i in range(2):
+            load_words(i, 1)
         nc.sync.dma_start(cen_sb[:], cen)
         nc.sync.dma_start(pos1_sb[:], pos1)
         nc.sync.dma_start(pos2_sb[:], pos2)
@@ -122,7 +123,7 @@ def tile_picked_gatedg_relu_e_kernel(
             a, b = cuts[i][c]
             nc.tensor.matmul_mx(
                 out=banks[i][c],
-                lhsT=(far_words[:, i, :] if g == 1 and c >= 2 else w_codes[i][g]).bitcast(FP4X4),
+                lhsT=(far_words[:, (i + 1) % 3, :] if g == 1 and c >= 2 else w_codes[i][g]).bitcast(FP4X4),
                 lhsT_scale=w_scales[:, i, g, :],
                 rhs=x_codes[g][:, a:b].bitcast(FP8X4),
                 rhs_scale=x_scales[g][:, a:b],
@@ -140,11 +141,11 @@ def tile_picked_gatedg_relu_e_kernel(
                 gather_v(first[:, : 2 * Q, j], j, near)
         for u in range(2):
             tiles = [keep.tile([P, 2, Q], F32, name="pair%d_%d" % (u, s), align_bytes=64) for s in range(2)]
-            order = [(s, e) for s in range(2) for e in range(2)] if u == 0 else [(s, e) for e in range(2) for s in range(2)]
+            order = [(s, e) for e in range(2) for s in range(2)]
             for s, e in order:
                 gather_s(tiles[s][:, e, :], 2 * u + e, (third, last)[s])
-            for tile, (a, b) in zip(tiles, (third, last)):
-                weave(copy_g, first[:, a:b, :], u, tile[:])
+            for tile, (a, b), copy in zip(tiles, (third, last), (copy_g, nc.scalar.copy if u else copy_g)):
+                weave(copy, first[:, a:b, :], u, tile[:])
 
         spans = [(s * Q, (s + 1) * Q) for s in range(4)]
         parts = [keep.tile([P, Q, PACK], BF16, name="second%d" % s, align_bytes=64) for s in range(4)]
@@ -175,10 +176,10 @@ def tile_picked_gatedg_relu_e_kernel(
             quantize(parts[s][:], 1, spans[s])
         nc.scalar.copy(
             far_words[:].rearrange("p i b -> p (i b)").bitcast(U32),
-            second_words[:].rearrange("p i b -> p (i b)").bitcast(U32),
+            late_words[:, 1:, :].rearrange("p i b -> p (i b)").bitcast(U32),
         )
         for c in range(2):
-            for i in (2, 1, 0):
+            for i in (1, 2, 0):
                 product(i, c, 1)
         for i, c in ((0, 3), (0, 2), (1, 2), (2, 2)):
             product(i, c, 1)

@@ -132,20 +132,21 @@ def tile_picked_gatedg_relu_e_kernel(
             )
 
         first = keep.tile([P, S, PACK], BF16, name="first", align_bytes=64)
-        trio = keep.tile([P, 3, 2 * Q], F32, name="trio", align_bytes=64)
+        trios = [keep.tile([P, 3, Q], F32, name="trio%d" % s, align_bytes=64) for s in range(2)]
+        pairs = [[keep.tile([P, 2, Q], F32, name="pair%d_%d" % (u, s), align_bytes=64) for s in range(2)] for u in range(2)]
+        for j in range(3):
+            for trio, span in zip(trios, (one, two)):
+                gather_v(trio[:, j, :], j, span)
         for j in range(PACK):
-            if j < 3:
-                gather_v(trio[:, j, :], j, near)
-            else:
-                nc.vector.tensor_copy(first[:, : 2 * Q, :3], trio[:].rearrange("p e n -> p n e"))
-                gather_v(first[:, : 2 * Q, j], j, near)
-        for u in range(2):
-            tiles = [keep.tile([P, 2, Q], F32, name="pair%d_%d" % (u, s), align_bytes=64) for s in range(2)]
-            order = [(s, e) for e in range(2) for s in range(2)]
-            for s, e in order:
-                gather_s(tiles[s][:, e, :], 2 * u + e, (third, last)[s])
-            for tile, (a, b), copy in zip(tiles, (third, last), (copy_g, nc.scalar.copy if u else copy_g)):
-                weave(copy, first[:, a:b, :], u, tile[:])
+            for s in (1, 0) if j < 2 else (0, 1):
+                gather_s(pairs[j // 2][s][:, j % 2, :], j, (third, last)[s])
+        weave(nc.vector.tensor_copy, first[:, 3 * Q :, :], 0, pairs[0][1][:])
+        weave(copy_g, first[:, 2 * Q : 3 * Q, :], 0, pairs[0][0][:])
+        for trio, (a, b) in zip(trios, (one, two)):
+            nc.vector.tensor_copy(first[:, a:b, :3], trio[:].rearrange("p e n -> p n e"))
+        gather_v(first[:, : 2 * Q, 3], 3, near)
+        weave(copy_g, first[:, 2 * Q : 3 * Q, :], 1, pairs[1][0][:])
+        weave(nc.scalar.copy, first[:, 3 * Q :, :], 1, pairs[1][1][:])
 
         spans = [(s * Q, (s + 1) * Q) for s in range(4)]
         parts = [keep.tile([P, Q, PACK], BF16, name="second%d" % s, align_bytes=64) for s in range(4)]

@@ -150,29 +150,32 @@ def tile_picked_gatedg_relu_e_kernel(
 
         spans = [(s * Q, (s + 1) * Q) for s in range(4)]
         parts = [keep.tile([P, Q, PACK], BF16, name="second%d" % s, align_bytes=64) for s in range(4)]
-        early = [keep.tile([P, 2, Q], F32, name="early%d" % s, align_bytes=64) for s in range(3)]
+        early = {s: keep.tile([P, 2, Q], F32, name="early%d" % s, align_bytes=64) for s in (1, 3)}
+        rows = keep.tile([P, 3, Q], F32, name="rows", align_bytes=64)
         late = keep.tile([P, 2, Q], F32, name="late", align_bytes=64)
-        for j in (4, 5):
-            gather_v(early[0][:, j % 2, :], j, (Q, 2 * Q))
-            gather_v(parts[0][:, :, j - PACK], j, spans[0])
-            gather_s(early[1][:, j % 2, :], j, third)
-            gather_s(early[2][:, j % 2, :], j, last)
-            if j == 4:
-                quantize(first[:], 0, (0, S))
-                for i in range(3):
-                    for c in range(len(cuts[i])):
-                        product(i, c, 0)
-        weave(nc.scalar.copy, parts[1][:], 0, early[0][:])
-        weave(copy_g, parts[2][:], 0, early[1][:])
-        weave(copy_g, parts[3][:], 0, early[2][:])
+        gather_v(early[1][:, 0, :], 4, two)
+        gather_v(parts[0][:, :, 0], 4, one)
+        gather_s(rows[:, 1, :], 4, third)
+        gather_s(early[3][:, 0, :], 4, last)
+        quantize(first[:], 0, (0, S))
+        for i in range(3):
+            for c in range(len(cuts[i])):
+                product(i, c, 0)
+        gather_v(rows[:, 2, :], 5, third)
+        gather_v(parts[0][:, :, 1], 5, one)
+        gather_s(early[1][:, 1, :], 5, two)
+        gather_s(early[3][:, 1, :], 5, last)
+        weave(nc.scalar.copy, parts[1][:], 0, early[1][:])
+        weave(copy_g, parts[2][:], 0, rows[:, 1:, :])
+        weave(copy_g, parts[3][:], 0, early[3][:])
         for j in (6, 7):
             for s in range(2):
                 gather_v(parts[s][:, :, j - PACK], j, spans[s])
             gather_s(late[:, j % 2, :], j, last)
-            gather_s(early[1][:, j % 2, :], j, third)
+            gather_s(rows[:, j % 2, :], j, third)
         weave(nc.scalar.copy, parts[3][:], 1, late[:])
         quantize(parts[0][:], 1, spans[0])
-        weave(nc.vector.tensor_copy, parts[2][:], 1, early[1][:])
+        weave(nc.vector.tensor_copy, parts[2][:], 1, rows[:, :2, :])
         for s in (1, 3, 2):
             quantize(parts[s][:], 1, spans[s])
         nc.scalar.copy(

@@ -38,7 +38,9 @@ def tile_picked_gatedg_relu_e_kernel(
         pos1_sb = keep.tile([P, V // PER_COL], U16, name="pos1_sb")
         pos2_sb = keep.tile([P, V // PER_COL], U16, name="pos2_sb")
 
-        planes = [keep.tile([P, T], F32, name="plane%d" % j, align_bytes=64)[:] for j in range(PASSES * PACK)]
+        opening = keep.tile([P, 2, T], F32, name="opening", align_bytes=64)
+        planes = [opening[:, j, :] for j in range(2)]
+        planes.extend(keep.tile([P, T], F32, name="plane%d" % j, align_bytes=64)[:] for j in range(2, PASSES * PACK))
         w_scales = keep.tile([P, 3, PASSES, N], U8, name="w_scales", align_bytes=64)
         late_words = keep.tile([P, 4, 2 * N], U8, name="late_words", align_bytes=64)
         far_words = keep.tile([P, 3, 2 * N], U8, name="far_words", align_bytes=64)
@@ -58,11 +60,11 @@ def tile_picked_gatedg_relu_e_kernel(
             rows = xT[g * K_PASS : (g + 1) * K_PASS, :].rearrange("(p j) t -> p j t", j=PACK)
             nc.sync.dma_start(planes[j], rows[:, j % PACK, :])
 
-        load_plane(0)
+        nc.sync.dma_start(opening[:], xT[:K_PASS, :].rearrange("(p j) t -> p j t", j=PACK)[:, :2, :])
         nc.sync.dma_start(offs_sb[:], offs)
         for i, scales in enumerate((w1_scales, w2_scales, w3_scales)):
             nc.sync.dma_start(w_scales[0:16, i, :, :].bitcast(I32), scales.rearrange("g r n -> r g n").bitcast(I32))
-        for j in range(1, 7):
+        for j in range(2, 7):
             load_plane(j)
         load_words(0, 0)
         for q in range(1, 4):
@@ -132,21 +134,20 @@ def tile_picked_gatedg_relu_e_kernel(
             )
 
         first = keep.tile([P, S, PACK], BF16, name="first", align_bytes=64)
-        trios = [keep.tile([P, 3, Q], F32, name="trio%d" % s, align_bytes=64) for s in range(2)]
-        pairs = [[keep.tile([P, 2, Q], F32, name="pair%d_%d" % (u, s), align_bytes=64) for s in range(2)] for u in range(2)]
-        for j in range(3):
-            for trio, span in zip(trios, (one, two)):
-                gather_v(trio[:, j, :], j, span)
+        trio = keep.tile([P, 3, 2 * Q], F32, name="trio", align_bytes=64)
         for j in range(PACK):
-            for s in (1, 0) if j < 2 else (0, 1):
-                gather_s(pairs[j // 2][s][:, j % 2, :], j, (third, last)[s])
-        weave(nc.vector.tensor_copy, first[:, 3 * Q :, :], 0, pairs[0][1][:])
-        weave(copy_g, first[:, 2 * Q : 3 * Q, :], 0, pairs[0][0][:])
-        for trio, (a, b) in zip(trios, (one, two)):
-            nc.vector.tensor_copy(first[:, a:b, :3], trio[:].rearrange("p e n -> p n e"))
-        gather_v(first[:, : 2 * Q, 3], 3, near)
-        weave(copy_g, first[:, 2 * Q : 3 * Q, :], 1, pairs[1][0][:])
-        weave(nc.scalar.copy, first[:, 3 * Q :, :], 1, pairs[1][1][:])
+            if j < 3:
+                gather_v(trio[:, j, :], j, near)
+            else:
+                nc.vector.tensor_copy(first[:, : 2 * Q, :3], trio[:].rearrange("p e n -> p n e"))
+                gather_v(first[:, : 2 * Q, j], j, near)
+        for u in range(2):
+            tiles = [keep.tile([P, 2, Q], F32, name="pair%d_%d" % (u, s), align_bytes=64) for s in range(2)]
+            order = [(s, e) for s in range(2) for e in range(2)] if u == 0 else [(s, e) for e in range(2) for s in range(2)]
+            for s, e in order:
+                gather_s(tiles[s][:, e, :], 2 * u + e, (third, last)[s])
+            for tile, (a, b), copy in zip(tiles, (third, last), (copy_g, nc.scalar.copy if u else copy_g)):
+                weave(copy, first[:, a:b, :], u, tile[:])
 
         spans = [(s * Q, (s + 1) * Q) for s in range(4)]
         parts = [keep.tile([P, Q, PACK], BF16, name="second%d" % s, align_bytes=64) for s in range(4)]

@@ -23,6 +23,7 @@ PASSES = K // K_PASS
 PER_COL = 16
 Q = S // 4
 HALF = V // 2
+LATE_SHARE = 192
 
 
 def tile_picked_gatedg_relu_e_kernel(
@@ -42,16 +43,15 @@ def tile_picked_gatedg_relu_e_kernel(
         planes = [opening[:, j, :] for j in range(2)]
         planes.extend(keep.tile([P, T], F32, name="plane%d" % j, align_bytes=64)[:] for j in range(2, PASSES * PACK))
         w_scales = keep.tile([P, 3, PASSES, N], U8, name="w_scales", align_bytes=64)
-        late_words = keep.tile([P, 4, 2 * N], U8, name="late_words", align_bytes=64)
-        far_words = keep.tile([P, 3, 2 * N], U8, name="far_words", align_bytes=64)
-        w_codes = [
-            [keep.tile([P, 2 * N], U8, name="w%d_codes" % i, align_bytes=64)[:], late_words[:, 2 + i, :]] for i in range(2)
-        ]
-        w_codes.append([late_words[:, g, :] for g in range(PASSES)])
+        early_words = keep.tile([P, 2 * N], U8, name="early_words", align_bytes=64)
+        late_words = keep.tile([P, 5, 2 * N], U8, name="late_words", align_bytes=64)
+        far_words = keep.tile([P, 4, 2 * N], U8, name="far_words", align_bytes=64)
+        rows = {(0, 1): 0, (1, 0): 1, (1, 1): 2, (2, 0): 3, (2, 1): 4}
         w_words = (w1_words, w2_words)
 
         def load_words(i, g):
-            nc.sync.dma_start(w_codes[i][g].bitcast(I32), w_words[i][g].bitcast(I32))
+            dst = late_words[:, rows[i, g], :] if (i, g) in rows else early_words[:]
+            nc.sync.dma_start(dst.bitcast(I32), w_words[i][g].bitcast(I32))
 
         nc.vector.memset(w_scales[:].bitcast(I32), 0)
 
@@ -74,7 +74,7 @@ def tile_picked_gatedg_relu_e_kernel(
             )
         load_plane(7)
         load_words(1, 0)
-        nc.sync.dma_start(late_words[:, :2, :].bitcast(I32), w3_words.rearrange("g p b -> p g b").bitcast(I32))
+        nc.sync.dma_start(late_words[:, 3:, :].bitcast(I32), w3_words.rearrange("g p b -> p g b").bitcast(I32))
         for i in range(2):
             load_words(i, 1)
         nc.sync.dma_start(cen_sb[:], cen)
@@ -123,9 +123,10 @@ def tile_picked_gatedg_relu_e_kernel(
 
         def product(i, c, g):
             a, b = cuts[i][c]
+            words = (far_words if c >= 2 and rows[i, g] < 4 else late_words)[:, rows[i, g], :] if (i, g) in rows else early_words[:]
             nc.tensor.matmul_mx(
                 out=banks[i][c],
-                lhsT=(far_words[:, (i + 1) % 3, :] if g == 1 and c >= 2 else w_codes[i][g]).bitcast(FP4X4),
+                lhsT=words.bitcast(FP4X4),
                 lhsT_scale=w_scales[:, i, g, :],
                 rhs=x_codes[g][:, a:b].bitcast(FP8X4),
                 rhs_scale=x_scales[g][:, a:b],
@@ -150,44 +151,31 @@ def tile_picked_gatedg_relu_e_kernel(
                 weave(copy, first[:, a:b, :], u, tile[:])
 
         spans = [(s * Q, (s + 1) * Q) for s in range(4)]
-        parts = [keep.tile([P, Q, PACK], BF16, name="second%d" % s, align_bytes=64) for s in range(4)]
-        early = {s: keep.tile([P, 2, Q], F32, name="early%d" % s, align_bytes=64) for s in (1, 3)}
-        rows = keep.tile([P, 3, Q], F32, name="rows", align_bytes=64)
-        late = keep.tile([P, 2, Q], F32, name="late", align_bytes=64)
-        gather_v(early[1][:, 0, :], 4, two)
-        gather_v(parts[0][:, :, 0], 4, one)
-        gather_s(rows[:, 1, :], 4, third)
-        gather_s(early[3][:, 0, :], 4, last)
-        quantize(first[:], 0, (0, S))
-        for i in range(3):
-            for c in range(len(cuts[i])):
-                product(i, c, 0)
-        gather_v(rows[:, 2, :], 5, third)
-        gather_v(parts[0][:, :, 1], 5, one)
-        gather_s(early[1][:, 1, :], 5, two)
-        gather_s(early[3][:, 1, :], 5, last)
-        weave(nc.scalar.copy, parts[1][:], 0, early[1][:])
-        weave(copy_g, parts[2][:], 0, rows[:, 1:, :])
-        weave(copy_g, parts[3][:], 0, early[3][:])
-        for j in (6, 7):
-            for s in range(2):
-                gather_v(parts[s][:, :, j - PACK], j, spans[s])
-            gather_s(late[:, j % 2, :], j, last)
-            gather_s(rows[:, j % 2, :], j, third)
-        weave(nc.scalar.copy, parts[3][:], 1, late[:])
-        quantize(parts[0][:], 1, spans[0])
-        weave(nc.vector.tensor_copy, parts[2][:], 1, rows[:, :2, :])
-        for s in (1, 3, 2):
-            quantize(parts[s][:], 1, spans[s])
+        second = keep.tile([P, S, PACK], BF16, name="second", align_bytes=64)
+        for j in range(PACK, 2 * PACK):
+            share = 2 * Q if j < 6 else LATE_SHARE
+            gather_v(second[:, :share, j - PACK], j, (0, share))
+            gather_s(second[:, share : 3 * Q, j - PACK], j, (share, 3 * Q))
+            gather_s(second[:, 3 * Q :, j - PACK], j, last)
+            if j == PACK:
+                quantize(first[:], 0, (0, S))
+                for i in range(3):
+                    for c in range(len(cuts[i]) if i == 0 else 2):
+                        product(i, c, 0)
+        for a, b in spans:
+            quantize(second[:, a:b, :], 1, (a, b))
         nc.scalar.copy(
             far_words[:].rearrange("p i b -> p (i b)").bitcast(U32),
-            late_words[:, 1:, :].rearrange("p i b -> p (i b)").bitcast(U32),
+            late_words[:, :4, :].rearrange("p i b -> p (i b)").bitcast(U32),
         )
         for c in range(2):
             for i in (1, 2, 0):
                 product(i, c, 1)
-        for i, c in ((0, 3), (0, 2), (1, 2), (2, 2)):
-            product(i, c, 1)
+        for c in (2, 3):
+            product(0, c, 1)
+        for i in (1, 2):
+            for g in range(PASSES):
+                product(i, 2, g)
 
         results = [keep.tile([P, S], F32, name=name) for name in ("y_sb", "e_sb", "h_sb")]
         y_sb, e_sb, h_sb = results
@@ -201,7 +189,7 @@ def tile_picked_gatedg_relu_e_kernel(
         empty(nc.vector.tensor_copy, 2, 0)
         for i in range(2):
             empty(nc.vector.tensor_copy, i, 1)
-        for c in (3, 2):
+        for c in (2, 3):
             empty(nc.scalar.copy, 0, c)
         empty(nc.scalar.copy, 2, 1)
         for i in (1, 2):

@@ -43,14 +43,14 @@ def tile_picked_gatedg_relu_e_kernel(
         planes = [opening[:, j, :] for j in range(2)]
         planes.extend(keep.tile([P, T], F32, name="plane%d" % j, align_bytes=64)[:] for j in range(2, PASSES * PACK))
         w_scales = keep.tile([P, 3, PASSES, N], U8, name="w_scales", align_bytes=64)
-        early_words = keep.tile([P, 2 * N], U8, name="early_words", align_bytes=64)
-        late_words = keep.tile([P, 5, 2 * N], U8, name="late_words", align_bytes=64)
-        far_words = keep.tile([P, 4, 2 * N], U8, name="far_words", align_bytes=64)
-        rows = {(0, 1): 0, (1, 0): 1, (1, 1): 2, (2, 0): 3, (2, 1): 4}
-        w_words = (w1_words, w2_words)
+        early_words = [keep.tile([P, 2 * N], U8, name="early_words%d" % i, align_bytes=64) for i in range(3)]
+        late_words = keep.tile([P, 3, 2 * N], U8, name="late_words", align_bytes=64)
+        far_words = keep.tile([P, 3, 2 * N], U8, name="far_words", align_bytes=64)
+        rows = {(0, 1): 0, (1, 1): 1, (2, 1): 2}
+        w_words = (w1_words, w2_words, w3_words)
 
         def load_words(i, g):
-            dst = late_words[:, rows[i, g], :] if (i, g) in rows else early_words[:]
+            dst = late_words[:, rows[i, g], :] if g else early_words[i][:]
             nc.sync.dma_start(dst.bitcast(I32), w_words[i][g].bitcast(I32))
 
         nc.vector.memset(w_scales[:].bitcast(I32), 0)
@@ -72,10 +72,10 @@ def tile_picked_gatedg_relu_e_kernel(
                 w_scales[32 * q : 32 * q + 4].rearrange("r i g n -> r (i g n)").bitcast(I32),
                 w_scales[4 * q : 4 * q + 4].rearrange("r i g n -> r (i g n)").bitcast(I32),
             )
-        load_plane(7)
         load_words(1, 0)
-        nc.sync.dma_start(late_words[:, 3:, :].bitcast(I32), w3_words.rearrange("g p b -> p g b").bitcast(I32))
-        for i in range(2):
+        load_plane(7)
+        load_words(2, 0)
+        for i in (2, 0, 1):
             load_words(i, 1)
         nc.sync.dma_start(cen_sb[:], cen)
         nc.sync.dma_start(pos1_sb[:], pos1)
@@ -123,7 +123,7 @@ def tile_picked_gatedg_relu_e_kernel(
 
         def product(i, c, g):
             a, b = cuts[i][c]
-            words = (far_words if c >= 2 and rows[i, g] < 4 else late_words)[:, rows[i, g], :] if (i, g) in rows else early_words[:]
+            words = (far_words if c >= 2 else late_words)[:, rows[i, g], :] if g else early_words[i][:]
             nc.tensor.matmul_mx(
                 out=banks[i][c],
                 lhsT=words.bitcast(FP4X4),
@@ -160,22 +160,19 @@ def tile_picked_gatedg_relu_e_kernel(
             if j == PACK:
                 quantize(first[:], 0, (0, S))
                 for i in range(3):
-                    for c in range(len(cuts[i]) if i == 0 else 2):
+                    for c in range(len(cuts[i])):
                         product(i, c, 0)
         for a, b in spans:
             quantize(second[:, a:b, :], 1, (a, b))
         nc.scalar.copy(
             far_words[:].rearrange("p i b -> p (i b)").bitcast(U32),
-            late_words[:, :4, :].rearrange("p i b -> p (i b)").bitcast(U32),
+            late_words[:].rearrange("p i b -> p (i b)").bitcast(U32),
         )
         for c in range(2):
             for i in (1, 2, 0):
                 product(i, c, 1)
-        for c in (2, 3):
-            product(0, c, 1)
-        for i in (1, 2):
-            for g in range(PASSES):
-                product(i, 2, g)
+        for i, c in ((0, 2), (0, 3), (1, 2), (2, 2)):
+            product(i, c, 1)
 
         results = [keep.tile([P, S], F32, name=name) for name in ("y_sb", "e_sb", "h_sb")]
         y_sb, e_sb, h_sb = results

@@ -23,7 +23,8 @@ PASSES = K // K_PASS
 PER_COL = 16
 Q = S // 4
 HALF = V // 2
-LATE_SHARE = 192
+EARLY_SPAN = (128, 416)
+LATE_SPAN = (160, 352)
 
 
 def tile_picked_gatedg_relu_e_kernel(
@@ -39,9 +40,9 @@ def tile_picked_gatedg_relu_e_kernel(
         pos1_sb = keep.tile([P, V // PER_COL], U16, name="pos1_sb")
         pos2_sb = keep.tile([P, V // PER_COL], U16, name="pos2_sb")
 
-        opening = keep.tile([P, 2, T], F32, name="opening", align_bytes=64)
-        planes = [opening[:, j, :] for j in range(2)]
-        planes.extend(keep.tile([P, T], F32, name="plane%d" % j, align_bytes=64)[:] for j in range(2, PASSES * PACK))
+        doubles = [keep.tile([P, 2, T], F32, name="double%d" % u, align_bytes=64) for u in range(2)]
+        planes = [doubles[j // 2][:, j % 2, :] for j in range(PACK)]
+        planes.extend(keep.tile([P, T], F32, name="plane%d" % j, align_bytes=64)[:] for j in range(PACK, PASSES * PACK))
         w_scales = keep.tile([P, 3, PASSES, N], U8, name="w_scales", align_bytes=64)
         early_words = [keep.tile([P, 2 * N], U8, name="early_words%d" % i, align_bytes=64) for i in range(3)]
         late_words = keep.tile([P, 3, 2 * N], U8, name="late_words", align_bytes=64)
@@ -60,11 +61,13 @@ def tile_picked_gatedg_relu_e_kernel(
             rows = xT[g * K_PASS : (g + 1) * K_PASS, :].rearrange("(p j) t -> p j t", j=PACK)
             nc.sync.dma_start(planes[j], rows[:, j % PACK, :])
 
-        nc.sync.dma_start(opening[:], xT[:K_PASS, :].rearrange("(p j) t -> p j t", j=PACK)[:, :2, :])
+        first_rows = xT[:K_PASS, :].rearrange("(p j) t -> p j t", j=PACK)
+        nc.sync.dma_start(doubles[0][:], first_rows[:, :2, :])
         nc.sync.dma_start(offs_sb[:], offs)
         for i, scales in enumerate((w1_scales, w2_scales, w3_scales)):
             nc.sync.dma_start(w_scales[0:16, i, :, :].bitcast(I32), scales.rearrange("g r n -> r g n").bitcast(I32))
-        for j in range(2, 7):
+        nc.sync.dma_start(doubles[1][:], first_rows[:, 2:, :])
+        for j in range(4, 7):
             load_plane(j)
         load_words(0, 0)
         for q in range(1, 4):
@@ -135,13 +138,12 @@ def tile_picked_gatedg_relu_e_kernel(
             )
 
         first = keep.tile([P, S, PACK], BF16, name="first", align_bytes=64)
-        trio = keep.tile([P, 3, 2 * Q], F32, name="trio", align_bytes=64)
-        for j in range(PACK):
-            if j < 3:
-                gather_v(trio[:, j, :], j, near)
-            else:
-                nc.vector.tensor_copy(first[:, : 2 * Q, :3], trio[:].rearrange("p e n -> p n e"))
-                gather_v(first[:, : 2 * Q, j], j, near)
+        duo = keep.tile([P, 2, 2 * Q], F32, name="duo", align_bytes=64)
+        for j in range(2):
+            gather_v(duo[:, j, :], j, near)
+        weave(nc.vector.tensor_copy, first[:, : 2 * Q, :], 0, duo[:])
+        for j in range(2, PACK):
+            gather_v(first[:, : 2 * Q, j], j, near)
         for u in range(2):
             tiles = [keep.tile([P, 2, Q], F32, name="pair%d_%d" % (u, s), align_bytes=64) for s in range(2)]
             order = [(s, e) for s in range(2) for e in range(2)] if u == 0 else [(s, e) for e in range(2) for s in range(2)]
@@ -153,10 +155,10 @@ def tile_picked_gatedg_relu_e_kernel(
         spans = [(s * Q, (s + 1) * Q) for s in range(4)]
         second = keep.tile([P, S, PACK], BF16, name="second", align_bytes=64)
         for j in range(PACK, 2 * PACK):
-            share = 2 * Q if j < 6 else LATE_SHARE
-            gather_v(second[:, :share, j - PACK], j, (0, share))
-            gather_s(second[:, share : 3 * Q, j - PACK], j, (share, 3 * Q))
-            gather_s(second[:, 3 * Q :, j - PACK], j, last)
+            a, b = EARLY_SPAN if j < 6 else LATE_SPAN
+            gather_s(second[:, :a, j - PACK], j, (0, a))
+            gather_v(second[:, a:b, j - PACK], j, (a, b))
+            gather_s(second[:, b:, j - PACK], j, (b, S))
             if j == PACK:
                 quantize(first[:], 0, (0, S))
                 for i in range(3):

@@ -23,7 +23,7 @@ PASSES = K // K_PASS
 PER_COL = 16
 Q = S // 4
 HALF = V // 2
-EARLY_SPAN = (128, 416)
+EARLY_SPAN = (160, 384)
 LATE_SPAN = (160, 352)
 
 
@@ -149,7 +149,7 @@ def tile_picked_gatedg_relu_e_kernel(
             order = [(s, e) for s in range(2) for e in range(2)] if u == 0 else [(s, e) for e in range(2) for s in range(2)]
             for s, e in order:
                 gather_s(tiles[s][:, e, :], 2 * u + e, (third, last)[s])
-            for tile, (a, b), copy in zip(tiles, (third, last), (copy_g, nc.scalar.copy if u else copy_g)):
+            for tile, (a, b), copy in zip(tiles, (third, last), (copy_g, copy_g)):
                 weave(copy, first[:, a:b, :], u, tile[:])
 
         spans = [(s * Q, (s + 1) * Q) for s in range(4)]

@@ -25,6 +25,7 @@ Q = S // 4
 HALF = V // 2
 EARLY_SPAN = (160, 384)
 LATE_SPAN = (160, 352)
+LAST_CUT = 416
 
 
 def tile_picked_gatedg_relu_e_kernel(
@@ -46,7 +47,7 @@ def tile_picked_gatedg_relu_e_kernel(
         w_scales = keep.tile([P, 3, PASSES, N], U8, name="w_scales", align_bytes=64)
         early_words = [keep.tile([P, 2 * N], U8, name="early_words%d" % i, align_bytes=64) for i in range(3)]
         late_words = keep.tile([P, 3, 2 * N], U8, name="late_words", align_bytes=64)
-        far_words = keep.tile([P, 3, 2 * N], U8, name="far_words", align_bytes=64)
+        far_words = keep.tile([P, 2, 2 * N], U8, name="far_words", align_bytes=64)
         rows = {(0, 1): 0, (1, 1): 1, (2, 1): 2}
         w_words = (w1_words, w2_words, w3_words)
 
@@ -67,7 +68,7 @@ def tile_picked_gatedg_relu_e_kernel(
         for i, scales in enumerate((w1_scales, w2_scales, w3_scales)):
             nc.sync.dma_start(w_scales[0:16, i, :, :].bitcast(I32), scales.rearrange("g r n -> r g n").bitcast(I32))
         nc.sync.dma_start(doubles[1][:], first_rows[:, 2:, :])
-        for j in range(4, 7):
+        for j in (4, 5):
             load_plane(j)
         load_words(0, 0)
         for q in range(1, 4):
@@ -75,6 +76,7 @@ def tile_picked_gatedg_relu_e_kernel(
                 w_scales[32 * q : 32 * q + 4].rearrange("r i g n -> r (i g n)").bitcast(I32),
                 w_scales[4 * q : 4 * q + 4].rearrange("r i g n -> r (i g n)").bitcast(I32),
             )
+        load_plane(6)
         load_words(1, 0)
         load_plane(7)
         load_words(2, 0)
@@ -96,10 +98,11 @@ def tile_picked_gatedg_relu_e_kernel(
         one, two = (0, Q), (Q, 2 * Q)
         cuts = [[one, two, third, last], [one, two, far], [one, two, far]]
         joint = [psum.tile([P, 3, Q], F32, name="joint%d" % s) for s in range(2)]
-        banks = [
-            [joint[c][:, i, :] if c < 2 else psum.tile([P, b - a], F32, name="bank%d_%d" % (i, a))[:] for c, (a, b) in enumerate(cuts[i])]
-            for i in range(3)
-        ]
+        far_bank = psum.tile([P, 2, 2 * Q], F32, name="far_bank")
+        banks = [[joint[c][:, i, :] for c in range(2)] for i in range(3)]
+        banks[0].extend(psum.tile([P, Q], F32, name="bank_y%d" % c)[:] for c in (2, 3))
+        for i in (1, 2):
+            banks[i].append(far_bank[:, i - 1, :])
 
         def picked(j, span):
             return planes[j].indirect(offs_sb[:, span[0] // PER_COL : span[1] // PER_COL])
@@ -126,15 +129,15 @@ def tile_picked_gatedg_relu_e_kernel(
 
         def product(i, c, g):
             a, b = cuts[i][c]
-            words = (far_words if c >= 2 else late_words)[:, rows[i, g], :] if g else early_words[i][:]
+            words = (far_words if c >= 2 and i < 2 else late_words)[:, rows[i, g], :] if g else early_words[i][:]
             nc.tensor.matmul_mx(
                 out=banks[i][c],
                 lhsT=words.bitcast(FP4X4),
                 lhsT_scale=w_scales[:, i, g, :],
                 rhs=x_codes[g][:, a:b].bitcast(FP8X4),
                 rhs_scale=x_scales[g][:, a:b],
-                start=(g == 0 and (c >= 2 or i == 0)),
-                stop=(g == PASSES - 1 and (c >= 2 or i == 0)),
+                start=(g == 0 and (i == 0 or (i, c) == (1, 2))),
+                stop=(g == PASSES - 1 and (i == 0 or (i, c) == (2, 2))),
             )
 
         first = keep.tile([P, S, PACK], BF16, name="first", align_bytes=64)
@@ -158,7 +161,8 @@ def tile_picked_gatedg_relu_e_kernel(
             a, b = EARLY_SPAN if j < 6 else LATE_SPAN
             gather_s(second[:, :a, j - PACK], j, (0, a))
             gather_v(second[:, a:b, j - PACK], j, (a, b))
-            gather_s(second[:, b:, j - PACK], j, (b, S))
+            for lo, hi in ((b, LAST_CUT), (LAST_CUT, S)) if j == 7 else ((b, S),):
+                gather_s(second[:, lo:hi, j - PACK], j, (lo, hi))
             if j == PACK:
                 quantize(first[:], 0, (0, S))
                 for i in range(3):
@@ -168,7 +172,7 @@ def tile_picked_gatedg_relu_e_kernel(
             quantize(second[:, a:b, :], 1, (a, b))
         nc.scalar.copy(
             far_words[:].rearrange("p i b -> p (i b)").bitcast(U32),
-            late_words[:].rearrange("p i b -> p (i b)").bitcast(U32),
+            late_words[:, :2, :].rearrange("p i b -> p (i b)").bitcast(U32),
         )
         for c in range(2):
             for i in (1, 2, 0):

@@ -41,12 +41,12 @@ def tile_picked_gatedg_relu_e_kernel(
         pos1_sb = keep.tile([P, V // PER_COL], U16, name="pos1_sb")
         pos2_sb = keep.tile([P, V // PER_COL], U16, name="pos2_sb")
 
-        doubles = [keep.tile([P, 2, T], F32, name="double%d" % u, align_bytes=64) for u in range(2)]
+        doubles = [keep.tile([P, 2, T], F32, name="double%d" % u, align_bytes=256) for u in range(2)]
         planes = [doubles[j // 2][:, j % 2, :] for j in range(PACK)]
-        planes.extend(keep.tile([P, T], F32, name="plane%d" % j, align_bytes=64)[:] for j in range(PACK, PASSES * PACK))
-        w_scales = keep.tile([P, 3, PASSES, N], U8, name="w_scales", align_bytes=64)
-        early_words = [keep.tile([P, 2 * N], U8, name="early_words%d" % i, align_bytes=64) for i in range(3)]
-        late_words = keep.tile([P, 3, 2 * N], U8, name="late_words", align_bytes=64)
+        planes.extend(keep.tile([P, T], F32, name="plane%d" % j, align_bytes=256)[:] for j in range(PACK, PASSES * PACK))
+        w_scales = keep.tile([P, 3, PASSES, N], U8, name="w_scales", align_bytes=256)
+        early_words = [keep.tile([P, 2 * N], U8, name="early_words%d" % i, align_bytes=256) for i in range(3)]
+        late_words = keep.tile([P, 3, 2 * N], U8, name="late_words", align_bytes=256)
         far_words = keep.tile([P, 2, 2 * N], U8, name="far_words", align_bytes=64)
         rows = {(0, 1): 0, (1, 1): 1, (2, 1): 2}
         w_words = (w1_words, w2_words, w3_words)
@@ -207,7 +207,7 @@ def tile_picked_gatedg_relu_e_kernel(
         passed = [[keep.tile([P, HALF], F32, name="passed%d_%d" % (c, d)) for d in range(2)] for c in range(2)]
         total = [keep.tile([P, HALF], F32, name="total%d" % c) for c in range(2)]
         h_pos2 = keep.tile([P, V], F32, name="h_pos2")
-        result = keep.tile([P, V], F32, name="result")
+        result = keep.tile([P, V], F32, name="result", align_bytes=256)
         for c in range(2):
             nc.scalar.activation(yc[c][:], y_sb[:].indirect(cen_sb[:, cols16[c]]), ACT.Copy)
         nc.scalar.activation(h_pos2[:], h_sb[:].indirect(pos2_sb[:]), ACT.Copy)

from contextlib import ExitStack

import concourse.mybir as mybir

K, T, S, V, N = 1024, 1024, 512, 256, 128
FLOPS = 3 * 2 * K * S * N

F32 = mybir.dt.float32
BF16 = mybir.dt.bfloat16
I32 = mybir.dt.int32
U32 = mybir.dt.uint32
U16 = mybir.dt.uint16
U8 = mybir.dt.uint8
FP8X4 = mybir.dt.float8_e4m3fn_x4
FP4X4 = mybir.dt.float4_e2m1fn_x4
ALU = mybir.AluOpType
ACT = mybir.ActivationFunctionType

P = 128
PACK = 4
K_PASS = P * PACK
PASSES = K // K_PASS
PER_COL = 16
Q = S // 4
HALF = V // 2
EARLY_SPAN = (160, 384)
LATE_SPAN = (160, 352)
LAST_CUT = 416


def tile_picked_gatedg_relu_e_kernel(
    tc, xT, w1_words, w1_scales, w2_words, w2_scales, w3_words, w3_scales, offs, cen, pos1, pos2, out
):
    nc = tc.nc
    with ExitStack() as ctx:
        keep = ctx.enter_context(tc.tile_pool(name="keep", bufs=1))
        psum = ctx.enter_context(tc.psum_pool(name="psum", bufs=1))

        offs_sb = keep.tile([P, S // PER_COL], U16, name="offs_sb")
        cen_sb = keep.tile([P, V // PER_COL], U16, name="cen_sb")
        pos1_sb = keep.tile([P, V // PER_COL], U16, name="pos1_sb")
        pos2_sb = keep.tile([P, V // PER_COL], U16, name="pos2_sb")

        doubles = [keep.tile([P, 2, T], F32, name="double%d" % u, align_bytes=256) for u in range(2)]
        planes = [doubles[j // 2][:, j % 2, :] for j in range(PACK)]
        planes.extend(keep.tile([P, T], F32, name="plane%d" % j, align_bytes=256)[:] for j in range(PACK, PASSES * PACK))
        w_scales = keep.tile([P, 3, PASSES, N], U8, name="w_scales", align_bytes=256)
        early_words = [keep.tile([P, 2 * N], U8, name="early_words%d" % i, align_bytes=256) for i in range(3)]
        late_words = keep.tile([P, 3, 2 * N], U8, name="late_words", align_bytes=256)
        far_words = keep.tile([P, 2, 2 * N], U8, name="far_words", align_bytes=64)
        rows = {(0, 1): 0, (1, 1): 1, (2, 1): 2}
        w_words = (w1_words, w2_words, w3_words)

        def load_words(i, g):
            dst = late_words[:, rows[i, g], :] if g else early_words[i][:]
            nc.sync.dma_start(dst.bitcast(I32), w_words[i][g].bitcast(I32))

        nc.vector.memset(w_scales[:].bitcast(I32), 0)

        def load_plane(j):
            g = j // PACK
            rows = xT[g * K_PASS : (g + 1) * K_PASS, :].rearrange("(p j) t -> p j t", j=PACK)
            nc.sync.dma_start(planes[j], rows[:, j % PACK, :])

        first_rows = xT[:K_PASS, :].rearrange("(p j) t -> p j t", j=PACK)
        nc.sync.dma_start(doubles[0][:], first_rows[:, :2, :])
        nc.sync.dma_start(offs_sb[:], offs)
        for i, scales in enumerate((w1_scales, w2_scales, w3_scales)):
            nc.sync.dma_start(w_scales[0:16, i, :, :].bitcast(I32), scales.rearrange("g r n -> r g n").bitcast(I32))
        nc.sync.dma_start(doubles[1][:], first_rows[:, 2:, :])
        for j in (4, 5):
            load_plane(j)
        load_words(0, 0)
        for q in range(1, 4):
            nc.sync.dma_start(
                w_scales[32 * q : 32 * q + 4].rearrange("r i g n -> r (i g n)").bitcast(I32),
                w_scales[4 * q : 4 * q + 4].rearrange("r i g n -> r (i g n)").bitcast(I32),
            )
        load_plane(6)
        load_words(1, 0)
        load_plane(7)
        load_words(2, 0)
        for i in (2, 0, 1):
            load_words(i, 1)
        nc.sync.dma_start(cen_sb[:], cen)
        nc.sync.dma_start(pos1_sb[:], pos1)
        nc.sync.dma_start(pos2_sb[:], pos2)

        warm_in = keep.tile([P, 8], F32, name="warm_in")
        warm_out = keep.tile([P, 8], F32, name="warm_out")
        nc.vector.memset(warm_in[:], 0.0)
        nc.scalar.activation(warm_out[:], warm_in[:], ACT.Sigmoid)

        x_codes = [keep.tile([P, S], U32, name="x_codes%d" % g, align_bytes=64) for g in range(PASSES)]
        x_scales = [keep.tile([P, S], U8, name="x_scales%d" % g, align_bytes=64) for g in range(PASSES)]

        near, far, third, last = (0, 2 * Q), (2 * Q, S), (2 * Q, 3 * Q), (3 * Q, S)
        one, two = (0, Q), (Q, 2 * Q)
        cuts = [[one, two, third, last], [one, two, far], [one, two, far]]
        joint = [psum.tile([P, 3, Q], F32, name="joint%d" % s) for s in range(2)]
        far_bank = psum.tile([P, 2, 2 * Q], F32, name="far_bank")
        banks = [[joint[c][:, i, :] for c in range(2)] for i in range(3)]
        banks[0].extend(psum.tile([P, Q], F32, name="bank_y%d" % c)[:] for c in (2, 3))
        for i in (1, 2):
            banks[i].append(far_bank[:, i - 1, :])

        def picked(j, span):
            return planes[j].indirect(offs_sb[:, span[0] // PER_COL : span[1] // PER_COL])

        def gather_v(dst, j, span):
            nc.vector.tensor_copy(dst, picked(j, span))

        def gather_s(dst, j, span):
            nc.scalar.activation(dst, picked(j, span), ACT.Copy)

        def copy_g(dst, src):
            nc.gpsimd.tensor_scalar(dst, src, 1.0, 0.0, ALU.mult, ALU.add)

        def weave(copy, dst, u, src):
            copy(dst[:, :, 2 * u : 2 * u + 2], src.rearrange("p e n -> p n e"))

        def quantize(src, g, span):
            a, b = span
            nc.vector.quantize_mx(
                out=x_codes[g][:, a:b].bitcast(FP8X4),
                scales=x_scales[g][:, a:b],
                in_=src.rearrange("p n t -> p (n t)"),
            )

        def product(i, c, g):
            a, b = cuts[i][c]
            words = (far_words if c >= 2 and i < 2 else late_words)[:, rows[i, g], :] if g else early_words[i][:]
            nc.tensor.matmul_mx(
                out=banks[i][c],
                lhsT=words.bitcast(FP4X4),
                lhsT_scale=w_scales[:, i, g, :],
                rhs=x_codes[g][:, a:b].bitcast(FP8X4),
                rhs_scale=x_scales[g][:, a:b],
                start=(g == 0 and (i == 0 or (i, c) == (1, 2))),
                stop=(g == PASSES - 1 and (i == 0 or (i, c) == (2, 2))),
            )

        first = keep.tile([P, S, PACK], BF16, name="first", align_bytes=64)
        duo = keep.tile([P, 2, 2 * Q], F32, name="duo", align_bytes=64)
        for j in range(2):
            gather_v(duo[:, j, :], j, near)
        weave(nc.vector.tensor_copy, first[:, : 2 * Q, :], 0, duo[:])
        for j in range(2, PACK):
            gather_v(first[:, : 2 * Q, j], j, near)
        for u in range(2):
            tiles = [keep.tile([P, 2, Q], F32, name="pair%d_%d" % (u, s), align_bytes=64) for s in range(2)]
            order = [(s, e) for s in range(2) for e in range(2)] if u == 0 else [(s, e) for e in range(2) for s in range(2)]
            for s, e in order:
                gather_s(tiles[s][:, e, :], 2 * u + e, (third, last)[s])
            for tile, (a, b), copy in zip(tiles, (third, last), (copy_g, copy_g)):
                weave(copy, first[:, a:b, :], u, tile[:])

        spans = [(s * Q, (s + 1) * Q) for s in range(4)]
        second = keep.tile([P, S, PACK], BF16, name="second", align_bytes=64)
        for j in range(PACK, 2 * PACK):
            a, b = EARLY_SPAN if j < 6 else LATE_SPAN
            gather_s(second[:, :a, j - PACK], j, (0, a))
            gather_v(second[:, a:b, j - PACK], j, (a, b))
            for lo, hi in ((b, LAST_CUT), (LAST_CUT, S)) if j == 7 else ((b, S),):
                gather_s(second[:, lo:hi, j - PACK], j, (lo, hi))
            if j == PACK:
                quantize(first[:], 0, (0, S))
                for i in range(3):
                    for c in range(len(cuts[i])):
                        product(i, c, 0)
        for a, b in spans:
            quantize(second[:, a:b, :], 1, (a, b))
        nc.scalar.copy(
            far_words[:].rearrange("p i b -> p (i b)").bitcast(U32),
            late_words[:, :2, :].rearrange("p i b -> p (i b)").bitcast(U32),
        )
        for c in range(2):
            for i in (1, 2, 0):
                product(i, c, 1)
        for i, c in ((0, 2), (0, 3), (1, 2), (2, 2)):
            product(i, c, 1)

        results = [keep.tile([P, S], F32, name=name) for name in ("y_sb", "e_sb", "h_sb")]
        y_sb, e_sb, h_sb = results

        def empty(copy, i, c):
            a, b = cuts[i][c]
            copy(results[i][:, a:b], banks[i][c])

        for i in range(2):
            empty(nc.scalar.copy, i, 0)
        empty(nc.vector.tensor_copy, 2, 0)
        for i in range(2):
            empty(nc.vector.tensor_copy, i, 1)
        for c in (2, 3):
            empty(nc.scalar.copy, 0, c)
        empty(nc.scalar.copy, 2, 1)
        for i in (1, 2):
            empty(nc.vector.tensor_copy, i, 2)

        halves = [slice(c * HALF, (c + 1) * HALF) for c in range(2)]
        cols16 = [slice(c * HALF // PER_COL, (c + 1) * HALF // PER_COL) for c in range(2)]
        lists = (pos1_sb, pos2_sb)
        yc = [keep.tile([P, HALF], F32, name="yc%d" % c) for c in range(2)]
        both = [[keep.tile([P, HALF], F32, name="both%d_%d" % (c, d)) for d in range(2)] for c in range(2)]
        gate = [[keep.tile([P, HALF], F32, name="gate%d_%d" % (c, d)) for d in range(2)] for c in range(2)]
        passed = [[keep.tile([P, HALF], F32, name="passed%d_%d" % (c, d)) for d in range(2)] for c in range(2)]
        total = [keep.tile([P, HALF], F32, name="total%d" % c) for c in range(2)]
        h_pos2 = keep.tile([P, V], F32, name="h_pos2")
        result = keep.tile([P, V], F32, name="result", align_bytes=256)
        for c in range(2):
            nc.scalar.activation(yc[c][:], y_sb[:].indirect(cen_sb[:, cols16[c]]), ACT.Copy)
        nc.scalar.activation(h_pos2[:], h_sb[:].indirect(pos2_sb[:]), ACT.Copy)
        early_e = keep.tile([P, HALF], F32, name="early_e")
        nc.vector.tensor_copy(early_e[:], e_sb[:].indirect(pos1_sb[:, cols16[1]]))
        for d in range(2):
            for c in range(2):
                source = early_e[:] if (c, d) == (1, 0) else e_sb[:].indirect(lists[d][:, cols16[c]])
                nc.vector.tensor_tensor(both[c][d][:], source, yc[c][:], ALU.add)
                nc.scalar.activation(gate[c][d][:], both[c][d][:], ACT.Sigmoid)
        for c in range(2):
            nc.vector.tensor_tensor(passed[c][0][:], h_sb[:].indirect(pos1_sb[:, cols16[c]]), gate[c][0][:], ALU.mult)
        for c in range(2):
            nc.vector.tensor_tensor(passed[c][1][:], h_pos2[:, halves[c]], gate[c][1][:], ALU.mult)
        for c in range(2):
            nc.vector.tensor_tensor(total[c][:], passed[c][0][:], passed[c][1][:], ALU.add)
        for c in range(2):
            nc.vector.tensor_scalar_max(result[:, halves[c]], total[c][:], 0.0)
        nc.sync.dma_start(out, result[:])
